import numpy as np
import ml_dtypes


def mxq(x, axis, fmt="e4m3"):
    dtype, down = {"e4m3": (ml_dtypes.float8_e4m3fn, 7), "e5m2": (ml_dtypes.float8_e5m2, 14)}[fmt]
    v = np.moveaxis(np.asarray(x, np.float32).astype(ml_dtypes.bfloat16).astype(np.float64), axis, -1)
    blocks = v.reshape(v.shape[:-1] + (-1, 32))
    amax = np.abs(blocks).max(-1, keepdims=True)
    byte = np.maximum(np.where(amax > 0, np.frexp(amax)[1] - 1 + 127, 0) - down, 1)
    scale = np.exp2(byte - 127.0)
    codes = (blocks / scale).astype(np.float32).astype(dtype).astype(np.float64)
    return np.moveaxis((codes * scale).reshape(v.shape), -1, axis)


WIDE = False


def mx_kscale(k):
    if not WIDE:
        return np.ones(k)
    levels = np.array([10, -10, 5, -5, 0])
    if k % 512:
        return np.exp2(np.random.permutation(np.resize(levels, k // 32))).repeat(32)
    a = np.empty((k // 512, 16))
    for p in range(k // 512):
        a[p, :8] = np.random.permutation(np.resize(levels, 8))
        for g in range(8):
            far = levels[np.abs(levels - a[p, g]) >= 10]
            a[p, g + 8] = far[np.random.randint(len(far))]
    return np.exp2(a.ravel()).repeat(32)


BF16 = ml_dtypes.bfloat16


def bf(x):
    return np.asarray(x, np.float32).astype(BF16)


def f64(x):
    return np.asarray(x).astype(np.float64)


E2M1 = np.array([0.0, 0.5, 1.0, 1.5, 2.0, 3.0, 4.0, 6.0, -0.0, -0.5, -1.0, -1.5, -2.0, -3.0, -4.0, -6.0])


def pack_weight(w, fmt):
    k, n = w.shape
    w = f64(bf(w)).reshape(k // 32, 32, n)
    amax = np.abs(w).max(1)
    if fmt == "e4m3":
        byte = np.frexp(amax)[1] - 1 + 127 - 7
    else:
        mant, ex = np.frexp(amax / 6.0)
        byte = np.where(mant > 0.5, ex, ex - 1) + 127
    byte = np.clip(np.where(amax > 0, byte, 1), 1, 254)
    scaled = (w * np.exp2(127.0 - byte)[:, None, :]).reshape(k, n).astype(np.float32)
    by_word = np.ascontiguousarray(scaled.reshape(k // 512, 128, 4, n).transpose(0, 1, 3, 2))
    if fmt == "e4m3":
        words = by_word.astype(ml_dtypes.float8_e4m3fn).view(np.uint8)
    else:
        c = by_word.astype(ml_dtypes.float4_e2m1fn).view(np.uint8) & 0xF
        words = c[..., 0::2] | (c[..., 1::2] << 4)
    return np.ascontiguousarray(words), np.ascontiguousarray(byte.astype(np.uint8).reshape(k // 512, 16, n))


def unpack_weight(words, scales, fmt):
    g, p, n, _ = words.shape
    if fmt == "e4m3":
        vals = np.ascontiguousarray(words).view(ml_dtypes.float8_e4m3fn).astype(np.float64)
    else:
        nib = np.empty((g, p, n, 4), np.uint8)
        nib[..., 0::2] = words & 0xF
        nib[..., 1::2] = words >> 4
        vals = E2M1[nib]
    vals = vals * np.repeat(np.exp2(scales.astype(np.float64) - 127.0), 8, axis=1)[..., None]
    return vals.transpose(0, 1, 3, 2).reshape(g * 512, n)
def pack4(w):
    words, scales = pack_weight(w, "e2m1")
    return words.reshape(words.shape[0], 128, -1), scales


def unpack4(words, scales):
    return unpack_weight(words.reshape(words.shape[0], 128, -1, 2), scales, "e2m1")


def planes(Y):
    n, m = Y.shape
    b = f64(bf(Y)).reshape(n // 32, 32, m)
    amax = np.abs(b).max(1)
    byte = np.clip(np.where(amax > 0, np.frexp(amax)[1] - 1 + 127 - 7, 1), 1, 254)
    codes = (b * np.exp2(127.0 - byte)[:, None, :]).reshape(n, m).astype(np.float32).astype(ml_dtypes.float8_e4m3fn).view(np.uint8)
    words = codes.reshape(n // 512, 128, 4, m).transpose(0, 1, 3, 2)
    return np.ascontiguousarray(words), np.ascontiguousarray(byte.astype(np.uint8).reshape(n // 512, 16, m))


P, M, R, S = 1536, 1024, 512, 512


def setup_inputs():
    r = mx_kscale(R)
    s = mx_kscale(S)
    t = mx_kscale(P)
    strength = np.exp(0.7 * np.random.randn(P))[:, None]
    left = np.random.randn(P, R) * P ** -0.25 * strength * r[None, :]
    right = np.random.randn(R, P) / np.sqrt(R) / r[:, None]
    measure = (0.5 + np.random.rand(P)) * t
    phi = np.random.randn(S, P) / np.sqrt(S) * s[:, None] / t[None, :]
    coef = 3.0 * P ** -0.25 * np.random.randn(S, M) / s[:, None]
    phi_words, phi_scales = pack4(phi)
    c_words, c_scales = pack_weight(coef, "e4m3")
    band = np.random.randn(P, 1)
    gap = 0.5 + 0.3 * np.abs(np.random.randn(P, M))
    energy = np.sqrt(band ** 2 + gap ** 2)
    half_beta = 0.5 + np.random.rand(M)
    source = 0.5 * strength * np.random.randn(P, M)
    return {"pair_left": bf(left), "pair_right": bf(right), "measure": bf(measure),
            "phi_words": phi_words, "phi_scales": phi_scales, "c_words": c_words, "c_scales": c_scales,
            "energy": bf(energy), "half_beta": bf(half_beta), "source": bf(source)}

def reference(pair_left, pair_right, measure, phi_words, phi_scales, c_words, c_scales, energy, half_beta, source):
    kern = (mxq(f64(pair_left), 1) @ mxq(f64(pair_right), 0)) * f64(measure)[None, :]
    delta = unpack4(phi_words, phi_scales).T @ unpack_weight(c_words, c_scales, "e4m3")
    e = f64(energy)
    chi = np.tanh(e * f64(half_beta)[None, :]) / (2.0 * e)
    y = (mxq(kern, 1) @ mxq(delta * chi, 0)) + f64(source)
    Y = y
    words, scales = planes(Y)
    return y, words, scales

@@ -1,0 +1,414 @@
+from contextlib import ExitStack
+
+import concourse.mybir as mybir
+from concourse.masks import make_identity
+
+F32 = mybir.dt.float32
+BF16 = mybir.dt.bfloat16
+I32 = mybir.dt.int32
+U32 = mybir.dt.uint32
+U8 = mybir.dt.uint8
+FP8X4 = mybir.dt.float8_e4m3fn_x4
+FP4X4 = mybir.dt.float4_e2m1fn_x4
+ACT = mybir.ActivationFunctionType
+ALU = mybir.AluOpType
+
+MOMENTA, SAMPLES, RANK, BASIS = 1536, 1024, 512, 512
+FLOPS = 2 * MOMENTA * (MOMENTA * RANK + BASIS * SAMPLES + MOMENTA * SAMPLES)
+
+P = 128
+PASS = 512
+GROUPS = MOMENTA // PASS
+CHUNK = 256
+CHUNKS = SAMPLES // CHUNK
+UNITS = CHUNKS * GROUPS
+
+KERN_START = 2
+KERN_EARLY = 2
+KERN_LATE = 2
+Y_LAG = 6
+SQ_EARLY = 2
+
+
+def tile_bcs_gap_sweep_k4_kernel(
+    tc, pair_left, pair_right, measure, phi_words, phi_scales, c_words, c_scales, energy, half_beta, source,
+    out_0, out_1, out_2,
+):
+    nc = tc.nc
+    with ExitStack() as ctx:
+        keep = ctx.enter_context(tc.tile_pool(name="keep", bufs=1))
+        flow = ctx.enter_context(tc.tile_pool(name="flow", bufs=2))
+        psum = ctx.enter_context(tc.psum_pool(name="psum", bufs=1))
+
+        def planes(name, width):
+            codes = keep.tile([P, width], U32, name=name + "_codes", align_bytes=64)
+            scales = keep.tile([P, width], U8, name=name + "_scales", align_bytes=64)
+            return codes, scales
+
+        def turn_bank(name):
+            return psum.tile([P, PASS], F32, name=name, tag="turn", bufs=3)
+
+        def first_bank(name):
+            return psum.tile([P, PASS], F32, name=name, tag="first", bufs=3)
+
+        ident = keep.tile([P, P], F32, name="ident")
+        make_identity(nc, ident[:])
+        phi_scale = keep.tile([P, MOMENTA], U8, name="phi_scale", align_bytes=64)
+        c_scale_raw = keep.tile([P, SAMPLES], U8, name="c_scale_raw", align_bytes=64)
+        nc.gpsimd.memset(phi_scale[:].bitcast(I32), 0)
+        nc.gpsimd.memset(c_scale_raw[:].bitcast(I32), 0)
+
+        right_raw, left_raw, e_sb, src_sb = {}, {}, {}, {}
+
+        def load_right(g):
+            right_raw[g] = flow.tile([P, 4, PASS], BF16, name="right_raw%d" % g, tag="raw", bufs=4)
+            nc.sync.dma_start(
+                out=right_raw[g][:],
+                in_=pair_right[:, PASS * g : PASS * (g + 1)].rearrange("(p j) c -> p j c", j=4),
+            )
+
+        def load_left(gi):
+            left_raw[gi] = flow.tile([P, 4, RANK], BF16, name="left_raw%d" % gi, tag="raw", bufs=4)
+            nc.sync.dma_start(
+                out=left_raw[gi][:],
+                in_=pair_left[PASS * gi : PASS * (gi + 1), :].rearrange("(p t) k -> p t k", t=4),
+            )
+
+        def load_energy(g, h):
+            e_sb[g, h] = keep.tile([P, 4, PASS], BF16, name="energy%d_%d" % (g, h))
+            nc.sync.dma_start(
+                out=e_sb[g, h][:],
+                in_=energy[PASS * g : PASS * (g + 1), PASS * h : PASS * (h + 1)].rearrange("(p t) m -> p t m", t=4),
+            )
+
+        def load_source(n):
+            c, gi = divmod(n, GROUPS)
+            src_sb[n] = flow.tile([P, 4, CHUNK], BF16, name="source%d" % n, tag="source", bufs=4)
+            nc.sync.dma_start(
+                out=src_sb[n][:],
+                in_=source[PASS * gi : PASS * (gi + 1), CHUNK * c : CHUNK * (c + 1)].rearrange("(p t) m -> p t m", t=4),
+            )
+
+        meas = keep.tile([P, GROUPS, 4], BF16, name="meas")
+        beta_raw = keep.tile([P, CHUNKS, 2], BF16, name="beta_raw")
+        beta = keep.tile([P, CHUNKS * 2], F32, name="beta")
+        phi = keep.tile([P, 2 * MOMENTA], U8, name="phi", align_bytes=64)
+        c_raw = keep.tile([P, SAMPLES], U32, name="c_raw", align_bytes=64)
+
+        right_q, left_q, kern_q, dc_q = {}, {}, {}, {}
+        grouped = {}
+
+        def quantise(src, dst):
+            nc.vector.quantize_mx(out=dst[0][:].bitcast(FP8X4), scales=dst[1][:], in_=src[:])
+
+        def wide_tile(name):
+            return flow.tile([P, 4 * PASS], BF16, name=name, tag="wide", bufs=4, align_bytes=64)
+
+        def interleave_right(g):
+            grouped["r", g] = wide_tile("right_wide%d" % g)
+            nc.vector.tensor_copy(
+                out=grouped["r", g][:].rearrange("p (t a b j) -> p a t b j", t=4, b=2, j=4),
+                in_=right_raw[g][:].rearrange("p j (a b t) -> p a t b j", b=2, t=4),
+            )
+
+        def quantise_right(g):
+            right_q[g] = planes("right%d" % g, PASS)
+            quantise(grouped["r", g], right_q[g])
+
+        def turn_left(gi):
+            grouped["l", gi] = wide_tile("left_wide%d" % gi)
+            words = left_raw[gi][:].rearrange("p t k -> p (t k)").bitcast(F32)
+            wide_words = grouped["l", gi][:].bitcast(F32)
+            for h in range(2):
+                bank = turn_bank("left_bank%d_%d" % (gi, h))
+                for a in range(4):
+                    t, u = 2 * h + a // 2, a % 2
+                    nc.tensor.transpose(bank[:, P * a : P * (a + 1)], words[:, 256 * t + u : 256 * (t + 1) : 2], ident[:])
+                nc.scalar.copy(
+                    out=wide_words[:, PASS * h : PASS * (h + 1)].rearrange("p (t i u) -> p t i u", t=2, u=2),
+                    in_=bank[:].rearrange("p (t u i) -> p t i u", t=2, u=2),
+                )
+
+        def quantise_left(gi):
+            left_q[gi] = planes("left%d" % gi, PASS)
+            quantise(grouped["l", gi], left_q[gi])
+
+        def kern_bank(n):
+            gi, g, s = n // 12, n // 4 % 3, n % 4
+            if s == 0:
+                grouped["k", g, gi] = wide_tile("kern_wide%d_%d" % (g, gi))
+            bank = first_bank("kern_bank%d" % n)
+            cols = slice(P * s, P * (s + 1))
+            for t in range(4):
+                nc.tensor.matmul_mx(
+                    out=bank[:, P * t : P * (t + 1)],
+                    lhsT=right_q[g][0][:, P * t : P * (t + 1)].bitcast(FP8X4),
+                    lhsT_scale=right_q[g][1][:, P * t : P * (t + 1)],
+                    rhs=left_q[gi][0][:, cols].bitcast(FP8X4),
+                    rhs_scale=left_q[gi][1][:, cols],
+                    start=True, stop=True,
+                )
+            nc.vector.tensor_tensor(
+                out=grouped["k", g, gi][:, PASS * s : PASS * (s + 1)].rearrange("p (i t) -> p i t", t=4),
+                in0=bank[:].rearrange("p (t i) -> p i t", t=4),
+                in1=meas[:, g, :].unsqueeze(1).to_broadcast([P, P, 4]),
+                op=ALU.mult,
+            )
+
+        def quantise_kern(q):
+            gi, g = divmod(q, GROUPS)
+            kern_q[g, gi] = planes("kern%d_%d" % (g, gi), PASS)
+            quantise(grouped["k", g, gi], kern_q[g, gi])
+
+        e_bank, inv, th, chi, delta, dct, dcw, y_bank, y_sb, y_bf = {}, {}, {}, {}, {}, {}, {}, {}, {}, {}
+
+        def turn_energy(n, use):
+            c, g = divmod(n, GROUPS)
+            words = e_sb[g, c // 2][:].rearrange("p t m -> p (t m)").bitcast(F32)
+            bank = turn_bank("e_bank%s%d" % (use, n))
+            for t in range(4):
+                at = 256 * t + P * (c % 2)
+                nc.tensor.transpose(bank[:, P * t : P * (t + 1)], words[:, at : at + P], ident[:])
+            e_bank[n] = bank[:].bitcast(BF16).rearrange("q (u b p e) -> q e u p b", u=2, b=2, e=2)
+
+        def in_word_order(ap):
+            return ap.rearrange("q (u p b) -> q u p b", u=2, b=2)
+
+        def inverse_root(n):
+            inv[n] = keep.tile([P, 2 * PASS], F32, name="inv%d" % n)
+            for e in range(2):
+                nc.scalar.activation(
+                    out=in_word_order(inv[n][:, PASS * e : PASS * (e + 1)]), in_=e_bank[n][:, e, :, :, :],
+                    func=ACT.Abs_reciprocal_sqrt, scale=2.0,
+                )
+
+        def square(n):
+            nc.scalar.activation(out=inv[n][:], in_=inv[n][:], func=ACT.Square)
+
+        def tanh(n):
+            c = n // GROUPS
+            for e in range(2):
+                th[n, e] = flow.tile([P, PASS], F32, name="tanh%d_%d" % (n, e), tag="tanh", bufs=4)
+                nc.scalar.activation(
+                    out=in_word_order(th[n, e][:]), in_=e_bank[n][:, e, :, :, :], func=ACT.Tanh,
+                    scale=beta[:, 2 * c + e : 2 * c + e + 1],
+                )
+
+        def weight(n):
+            for e in range(2):
+                chi[n, e] = flow.tile([P, PASS], F32, name="chi%d_%d" % (n, e), tag="chi", bufs=2)
+                nc.gpsimd.tensor_tensor(
+                    out=chi[n, e][:], in0=th[n, e][:], in1=inv[n][:, PASS * e : PASS * (e + 1)], op=ALU.mult
+                )
+
+        def weighted_gap(n):
+            c, g = divmod(n, GROUPS)
+            dct[n] = flow.tile([P, 2 * PASS], BF16, name="dct%d" % n, tag="dct", bufs=2)
+            for e in range(2):
+                bank = first_bank("delta_bank%d_%d" % (n, e))
+                cols = slice(CHUNK * c + P * e, CHUNK * c + P * (e + 1))
+                nc.tensor.matmul_mx(
+                    out=bank[:],
+                    lhsT=c_q[0][:, cols].bitcast(FP8X4),
+                    lhsT_scale=c_q[1][:, cols],
+                    rhs=phi[:, 2 * PASS * g : 2 * PASS * (g + 1)].bitcast(FP4X4),
+                    rhs_scale=phi_scale[:, PASS * g : PASS * (g + 1)],
+                    start=True, stop=True,
+                )
+                nc.vector.tensor_tensor(
+                    out=in_word_order(dct[n][:, PASS * e : PASS * (e + 1)]),
+                    in0=bank[:].rearrange("q (p u b) -> q u p b", u=2, b=2),
+                    in1=in_word_order(chi[n, e][:]),
+                    op=ALU.mult,
+                )
+
+        def turn_back(n):
+            words = dct[n][:].bitcast(F32)
+            bank = turn_bank("back_bank%d" % n)
+            for a in range(4):
+                nc.tensor.transpose(bank[:, P * a : P * (a + 1)], words[:, P * a : P * (a + 1)], ident[:])
+            dcw[n] = flow.tile([P, 4 * CHUNK], BF16, name="dcw%d" % n, tag="dcw", bufs=2, align_bytes=64)
+            nc.scalar.copy(
+                out=dcw[n][:].bitcast(F32).rearrange("p (q a) -> p q a", a=4),
+                in_=bank[:].rearrange("p (a q) -> p q a", a=4),
+            )
+
+        def quantise_gap(n):
+            dc_q[n] = planes("dc%d" % n, CHUNK)
+            quantise(dcw[n], dc_q[n])
+
+        y_scale_first = keep.tile([P, SAMPLES], U8, name="y_scale_first", align_bytes=64)
+        y_scale_rest = keep.tile([P, SAMPLES], U8, name="y_scale_rest", align_bytes=64)
+
+        def new_gap(n):
+            c, gi = divmod(n, GROUPS)
+            y_sb[n] = flow.tile([P, 4, CHUNK], F32, name="y%d" % n, tag="y", bufs=3)
+            for h in range(2):
+                bank = psum.tile([P, PASS], F32, name="y_bank%d_%d" % (n, h), tag="second", bufs=2)
+                for a in range(2):
+                    cols = slice(P * (2 * h + a), P * (2 * h + a + 1))
+                    for g in range(GROUPS):
+                        nc.tensor.matmul_mx(
+                            out=bank[:, CHUNK * a : CHUNK * (a + 1)],
+                            lhsT=kern_q[g, gi][0][:, cols].bitcast(FP8X4),
+                            lhsT_scale=kern_q[g, gi][1][:, cols],
+                            rhs=dc_q[GROUPS * c + g][0][:].bitcast(FP8X4),
+                            rhs_scale=dc_q[GROUPS * c + g][1][:],
+                            start=(g == 0), stop=(g == GROUPS - 1),
+                        )
+                nc.vector.tensor_tensor(
+                    out=y_sb[n][:, 2 * h : 2 * h + 2, :],
+                    in0=bank[:].rearrange("p (a m) -> p a m", a=2),
+                    in1=src_sb[n][:, 2 * h : 2 * h + 2, :],
+                    op=ALU.add,
+                )
+            nc.sync.dma_start(
+                out=out_0[PASS * gi : PASS * (gi + 1), CHUNK * c : CHUNK * (c + 1)].rearrange("(p t) m -> p t m", t=4),
+                in_=y_sb[n][:],
+            )
+
+        def round_y(n):
+            y_bf[n] = flow.tile([P, 4 * CHUNK], BF16, name="y_bf%d" % n, tag="y_bf", bufs=2, align_bytes=64)
+            nc.scalar.copy(
+                out=y_bf[n][:].rearrange("p (c i t) -> p c t i", i=2, t=4),
+                in_=y_sb[n][:].rearrange("p t (c i) -> p c t i", i=2),
+            )
+
+        def quantise_y(n):
+            c, gi = divmod(n, GROUPS)
+            cols = slice(CHUNK * c, CHUNK * (c + 1))
+            codes = flow.tile([P, CHUNK], U32, name="y_codes%d" % n, tag="y_codes", bufs=3, align_bytes=64)
+            scales = y_scale_first[:, cols] if gi == 0 else y_scale_rest[4 * (gi - 1) :, cols]
+            nc.vector.quantize_mx(out=codes[:].bitcast(FP8X4), scales=scales, in_=y_bf[n][:])
+            nc.sync.dma_start(
+                out=out_1[gi].rearrange("p m t -> p (m t)").bitcast(I32)[:, cols], in_=codes[:].bitcast(I32)
+            )
+            if c == CHUNKS - 1 and gi == 0:
+                for q in range(4):
+                    nc.sync.dma_start(
+                        out=out_2[0, 4 * q : 4 * q + 4, :].bitcast(I32),
+                        in_=y_scale_first[32 * q : 32 * q + 4, :].bitcast(I32),
+                    )
+            if c == CHUNKS - 1 and gi == GROUPS - 1:
+                for q in range(4):
+                    nc.sync.dma_start(
+                        out=out_2[1:, 4 * q : 4 * q + 4, :].bitcast(I32),
+                        in_=y_scale_rest[32 * q : 32 * q + 8, :].bitcast(I32),
+                    )
+
+        c_q = planes("coef", SAMPLES)
+
+        def sort_coefficients():
+            nc.vector.tensor_copy(
+                out=c_q[0][:].bitcast(I32).rearrange("p (c e a b) -> p c a e b", c=CHUNKS, e=2, b=4),
+                in_=c_raw[:].bitcast(I32).rearrange("p (c a b e) -> p c a e b", c=CHUNKS, e=2, b=4),
+            )
+            nc.vector.tensor_copy(
+                out=c_q[1][:].rearrange("p (c e a b) -> p c a e b", c=CHUNKS, e=2, b=16),
+                in_=c_scale_raw[:].rearrange("p (c a b e) -> p c a e b", c=CHUNKS, e=2, b=16),
+            )
+
+        kern_done = []
+        kern_total = 12 * GROUPS
+
+        def kern_banks(count):
+            for n in range(len(kern_done), min(len(kern_done) + count, kern_total)):
+                kern_bank(n)
+                kern_done.append(n)
+
+        kern_quantised = []
+
+        def kern_quantise_ready(lag):
+            for q in range(len(kern_quantised), (len(kern_done) - lag) // 4):
+                quantise_kern(q)
+                kern_quantised.append(q)
+
+        order = [GROUPS * (2 * h + cc) + g for h in range(2) for g in range(GROUPS) for cc in range(2)]
+        with tc.manual_schedule(engines={mybir.EngineType.Activation, mybir.EngineType.SP}):
+            load_right(0)
+            load_energy(0, 0)
+            load_left(0)
+            nc.sync.dma_start(out=meas[:], in_=measure.rearrange("(g p t) -> p g t", p=P, t=4))
+            load_right(1)
+            load_energy(1, 0)
+            load_right(2)
+            load_energy(2, 0)
+            load_energy(0, 1)
+            interleave_right(0)
+            turn_energy(order[0], "a")
+            for step, n in enumerate(order):
+                inverse_root(n)
+                if step == 0:
+                    turn_left(0)
+                if step + 1 < UNITS:
+                    turn_energy(order[step + 1], "a")
+                if step == 0:
+                    interleave_right(1)
+                    quantise_right(0)
+                    load_left(1)
+                    load_energy(1, 1)
+                    load_energy(2, 1)
+                    quantise_left(0)
+                if step == 1:
+                    interleave_right(2)
+                    quantise_right(1)
+                    load_left(2)
+                    nc.sync.dma_start(out=beta_raw[:], in_=half_beta.rearrange("(c q e) -> q c e", q=P, e=2))
+                    nc.sync.dma_start(out=c_raw[:].bitcast(I32), in_=c_words[0].rearrange("p n t -> p (n t)").bitcast(I32))
+                    for q in range(4):
+                        nc.sync.dma_start(
+                            out=c_scale_raw[32 * q : 32 * q + 4, :].bitcast(I32),
+                            in_=c_scales[0, 4 * q : 4 * q + 4, :].bitcast(I32),
+                        )
+                    for q in range(4):
+                        nc.sync.dma_start(
+                            out=phi_scale[32 * q : 32 * q + 4, :].bitcast(I32),
+                            in_=phi_scales[0, 4 * q : 4 * q + 4, :].bitcast(I32),
+                        )
+                    nc.sync.dma_start(out=phi[:].bitcast(I32), in_=phi_words[0].bitcast(I32))
+                if step >= KERN_START:
+                    kern_banks(KERN_EARLY)
+                if step == KERN_START:
+                    quantise_right(2)
+                if step == 6:
+                    turn_left(1)
+                if step == 7:
+                    quantise_left(1)
+                if step == 9:
+                    turn_left(2)
+                if step == 10:
+                    quantise_left(2)
+                kern_quantise_ready(1)
+            nc.scalar.copy(out=beta[:], in_=beta_raw[:].rearrange("q c e -> q (c e)"))
+            sort_coefficients()
+            for n in range(4):
+                load_source(n)
+
+        for n in range(SQ_EARLY):
+            square(n)
+        turn_energy(0, "b")
+        for step in range(UNITS + Y_LAG + 2):
+            if step < UNITS:
+                tanh(step)
+            if step + 1 < UNITS:
+                turn_energy(step + 1, "b")
+            if 0 <= step - 2 < UNITS:
+                turn_back(step - 2)
+            if 0 <= step - 1 < UNITS:
+                weighted_gap(step - 1)
+            if step < UNITS:
+                weight(step)
+            if step + SQ_EARLY < UNITS:
+                square(step + SQ_EARLY)
+            if 0 <= step - Y_LAG < UNITS:
+                new_gap(step - Y_LAG)
+                if step - Y_LAG + 4 < UNITS:
+                    load_source(step - Y_LAG + 4)
+            kern_banks(KERN_LATE)
+            if 0 <= step - 2 < UNITS:
+                quantise_gap(step - 2)
+            if 0 <= step - Y_LAG - 1 < UNITS:
+                quantise_y(step - Y_LAG - 1)
+            kern_quantise_ready(0)
+            if 0 <= step - Y_LAG < UNITS:
+                round_y(step - Y_LAG)

@@ -23,11 +23,31 @@ CHUNK = 256
 CHUNKS = SAMPLES // CHUNK
 UNITS = CHUNKS * GROUPS
 
-KERN_START = 2
-KERN_EARLY = 2
-KERN_LATE = 2
-Y_LAG = 6
+KERN_START = 1
+KERN_EARLY = 1.6
+KERN_LATE = 1.8
+Y_LAG = 5
 SQ_EARLY = 2
+BIG = 13
+LEFT_S = (0, 1, 2,)
+L1 = 5
+L2 = 12
+CSORT = 9
+R_LAG = 7
+THB = 2
+JUMP = 3
+LASTV = 1
+R2 = 2
+OPEN = 0
+LOADS = "R0 L0 E00 m R1 E10 R2 E20 L1 E01 E11 E21 s L2"
+L0 = 0
+R1 = 1
+SQ_RATE = 1
+Y2 = 11
+G_COLS = 896
+RIGHT_S = ()
+R_RATE = 1.3
+R_OFF = 1
 
 
 def tile_bcs_gap_sweep_k4_kernel(
@@ -39,17 +59,15 @@ def tile_bcs_gap_sweep_k4_kernel(
         keep = ctx.enter_context(tc.tile_pool(name="keep", bufs=1))
         flow = ctx.enter_context(tc.tile_pool(name="flow", bufs=2))
         psum = ctx.enter_context(tc.psum_pool(name="psum", bufs=1))
+        ctx.enter_context(tc.manual_schedule())
 
         def planes(name, width):
             codes = keep.tile([P, width], U32, name=name + "_codes", align_bytes=64)
             scales = keep.tile([P, width], U8, name=name + "_scales", align_bytes=64)
             return codes, scales
 
-        def turn_bank(name):
-            return psum.tile([P, PASS], F32, name=name, tag="turn", bufs=3)
-
-        def first_bank(name):
-            return psum.tile([P, PASS], F32, name=name, tag="first", bufs=3)
+        def new_bank(name):
+            return psum.tile([P, PASS], F32, name=name, tag="ring", bufs=8)
 
         ident = keep.tile([P, P], F32, name="ident")
         make_identity(nc, ident[:])
@@ -61,14 +79,14 @@ def tile_bcs_gap_sweep_k4_kernel(
         right_raw, left_raw, e_sb, src_sb = {}, {}, {}, {}
 
         def load_right(g):
-            right_raw[g] = flow.tile([P, 4, PASS], BF16, name="right_raw%d" % g, tag="raw", bufs=4)
+            right_raw[g] = flow.tile([P, 4, PASS], BF16, name="right_raw%d" % g, tag="raw", bufs=6)
             nc.sync.dma_start(
                 out=right_raw[g][:],
                 in_=pair_right[:, PASS * g : PASS * (g + 1)].rearrange("(p j) c -> p j c", j=4),
             )
 
         def load_left(gi):
-            left_raw[gi] = flow.tile([P, 4, RANK], BF16, name="left_raw%d" % gi, tag="raw", bufs=4)
+            left_raw[gi] = flow.tile([P, 4, RANK], BF16, name="left_raw%d" % gi, tag="raw", bufs=6)
             nc.sync.dma_start(
                 out=left_raw[gi][:],
                 in_=pair_left[PASS * gi : PASS * (gi + 1), :].rearrange("(p t) k -> p t k", t=4),
@@ -81,12 +99,11 @@ def tile_bcs_gap_sweep_k4_kernel(
                 in_=energy[PASS * g : PASS * (g + 1), PASS * h : PASS * (h + 1)].rearrange("(p t) m -> p t m", t=4),
             )
 
-        def load_source(n):
-            c, gi = divmod(n, GROUPS)
-            src_sb[n] = flow.tile([P, 4, CHUNK], BF16, name="source%d" % n, tag="source", bufs=4)
+        def load_source(gi, h):
+            src_sb[gi, h] = flow.tile([P, 4, PASS], BF16, name="source%d_%d" % (gi, h), tag="raw", bufs=6)
             nc.sync.dma_start(
-                out=src_sb[n][:],
-                in_=source[PASS * gi : PASS * (gi + 1), CHUNK * c : CHUNK * (c + 1)].rearrange("(p t) m -> p t m", t=4),
+                out=src_sb[gi, h][:],
+                in_=source[PASS * gi : PASS * (gi + 1), PASS * h : PASS * (h + 1)].rearrange("(p t) m -> p t m", t=4),
             )
 
         meas = keep.tile([P, GROUPS, 4], BF16, name="meas")
@@ -106,7 +123,7 @@ def tile_bcs_gap_sweep_k4_kernel(
 
         def interleave_right(g):
             grouped["r", g] = wide_tile("right_wide%d" % g)
-            nc.vector.tensor_copy(
+            (nc.scalar.copy if g in RIGHT_S else nc.vector.tensor_copy)(
                 out=grouped["r", g][:].rearrange("p (t a b j) -> p a t b j", t=4, b=2, j=4),
                 in_=right_raw[g][:].rearrange("p j (a b t) -> p a t b j", b=2, t=4),
             )
@@ -120,11 +137,11 @@ def tile_bcs_gap_sweep_k4_kernel(
             words = left_raw[gi][:].rearrange("p t k -> p (t k)").bitcast(F32)
             wide_words = grouped["l", gi][:].bitcast(F32)
             for h in range(2):
-                bank = turn_bank("left_bank%d_%d" % (gi, h))
+                bank = new_bank("left_bank%d_%d" % (gi, h))
                 for a in range(4):
                     t, u = 2 * h + a // 2, a % 2
                     nc.tensor.transpose(bank[:, P * a : P * (a + 1)], words[:, 256 * t + u : 256 * (t + 1) : 2], ident[:])
-                nc.scalar.copy(
+                (nc.scalar.copy if gi in LEFT_S else nc.vector.tensor_copy)(
                     out=wide_words[:, PASS * h : PASS * (h + 1)].rearrange("p (t i u) -> p t i u", t=2, u=2),
                     in_=bank[:].rearrange("p (t u i) -> p t i u", t=2, u=2),
                 )
@@ -137,7 +154,7 @@ def tile_bcs_gap_sweep_k4_kernel(
             gi, g, s = n // 12, n // 4 % 3, n % 4
             if s == 0:
                 grouped["k", g, gi] = wide_tile("kern_wide%d_%d" % (g, gi))
-            bank = first_bank("kern_bank%d" % n)
+            bank = new_bank("kern_bank%d" % n)
             cols = slice(P * s, P * (s + 1))
             for t in range(4):
                 nc.tensor.matmul_mx(
@@ -160,12 +177,13 @@ def tile_bcs_gap_sweep_k4_kernel(
             kern_q[g, gi] = planes("kern%d_%d" % (g, gi), PASS)
             quantise(grouped["k", g, gi], kern_q[g, gi])
 
+        back = {}
         e_bank, inv, th, chi, delta, dct, dcw, y_bank, y_sb, y_bf = {}, {}, {}, {}, {}, {}, {}, {}, {}, {}
 
         def turn_energy(n, use):
             c, g = divmod(n, GROUPS)
             words = e_sb[g, c // 2][:].rearrange("p t m -> p (t m)").bitcast(F32)
-            bank = turn_bank("e_bank%s%d" % (use, n))
+            bank = new_bank("e_bank%s%d" % (use, n))
             for t in range(4):
                 at = 256 * t + P * (c % 2)
                 nc.tensor.transpose(bank[:, P * t : P * (t + 1)], words[:, at : at + P], ident[:])
@@ -175,7 +193,7 @@ def tile_bcs_gap_sweep_k4_kernel(
             return ap.rearrange("q (u p b) -> q u p b", u=2, b=2)
 
         def inverse_root(n):
-            inv[n] = keep.tile([P, 2 * PASS], F32, name="inv%d" % n)
+            inv[n] = flow.tile([P, 2 * PASS], F32, name="inv%d" % n, tag="big", bufs=BIG)
             for e in range(2):
                 nc.scalar.activation(
                     out=in_word_order(inv[n][:, PASS * e : PASS * (e + 1)]), in_=e_bank[n][:, e, :, :, :],
@@ -187,25 +205,27 @@ def tile_bcs_gap_sweep_k4_kernel(
 
         def tanh(n):
             c = n // GROUPS
+            th[n] = flow.tile([P, 2 * PASS], F32, name="tanh%d" % n, tag="tanh", bufs=THB)
             for e in range(2):
-                th[n, e] = flow.tile([P, PASS], F32, name="tanh%d_%d" % (n, e), tag="tanh", bufs=4)
                 nc.scalar.activation(
-                    out=in_word_order(th[n, e][:]), in_=e_bank[n][:, e, :, :, :], func=ACT.Tanh,
+                    out=in_word_order(th[n][:, PASS * e : PASS * (e + 1)]), in_=e_bank[n][:, e, :, :, :], func=ACT.Tanh,
                     scale=beta[:, 2 * c + e : 2 * c + e + 1],
                 )
 
         def weight(n):
-            for e in range(2):
-                chi[n, e] = flow.tile([P, PASS], F32, name="chi%d_%d" % (n, e), tag="chi", bufs=2)
-                nc.gpsimd.tensor_tensor(
-                    out=chi[n, e][:], in0=th[n, e][:], in1=inv[n][:, PASS * e : PASS * (e + 1)], op=ALU.mult
-                )
+            chi[n] = flow.tile([P, 2 * PASS], F32, name="chi%d" % n, tag="turns", bufs=3, align_bytes=64)
+            if G_COLS > 0:
+                nc.gpsimd.tensor_tensor(out=chi[n][:, :G_COLS], in0=th[n][:, :G_COLS], in1=inv[n][:, :G_COLS], op=ALU.mult)
+
+        def weight_rest(n):
+            if G_COLS < 1024:
+                nc.vector.tensor_tensor(out=chi[n][:, G_COLS:], in0=th[n][:, G_COLS:], in1=inv[n][:, G_COLS:], op=ALU.mult)
 
         def weighted_gap(n):
             c, g = divmod(n, GROUPS)
             dct[n] = flow.tile([P, 2 * PASS], BF16, name="dct%d" % n, tag="dct", bufs=2)
             for e in range(2):
-                bank = first_bank("delta_bank%d_%d" % (n, e))
+                bank = new_bank("delta_bank%d_%d" % (n, e))
                 cols = slice(CHUNK * c + P * e, CHUNK * c + P * (e + 1))
                 nc.tensor.matmul_mx(
                     out=bank[:],
@@ -218,16 +238,20 @@ def tile_bcs_gap_sweep_k4_kernel(
                 nc.vector.tensor_tensor(
                     out=in_word_order(dct[n][:, PASS * e : PASS * (e + 1)]),
                     in0=bank[:].rearrange("q (p u b) -> q u p b", u=2, b=2),
-                    in1=in_word_order(chi[n, e][:]),
+                    in1=in_word_order(chi[n][:, PASS * e : PASS * (e + 1)]),
                     op=ALU.mult,
                 )
 
         def turn_back(n):
             words = dct[n][:].bitcast(F32)
-            bank = turn_bank("back_bank%d" % n)
+            bank = new_bank("back_bank%d" % n)
             for a in range(4):
                 nc.tensor.transpose(bank[:, P * a : P * (a + 1)], words[:, P * a : P * (a + 1)], ident[:])
-            dcw[n] = flow.tile([P, 4 * CHUNK], BF16, name="dcw%d" % n, tag="dcw", bufs=2, align_bytes=64)
+            back[n] = bank
+
+        def copy_back(n):
+            bank = back[n]
+            dcw[n] = flow.tile([P, 4 * CHUNK], BF16, name="dcw%d" % n, tag="turns", bufs=3, align_bytes=64)
             nc.scalar.copy(
                 out=dcw[n][:].bitcast(F32).rearrange("p (q a) -> p q a", a=4),
                 in_=bank[:].rearrange("p (a q) -> p q a", a=4),
@@ -240,26 +264,37 @@ def tile_bcs_gap_sweep_k4_kernel(
         y_scale_first = keep.tile([P, SAMPLES], U8, name="y_scale_first", align_bytes=64)
         y_scale_rest = keep.tile([P, SAMPLES], U8, name="y_scale_rest", align_bytes=64)
 
+        def y_pass(n, h, a, g):
+            c, gi = divmod(n, GROUPS)
+            cols = slice(P * (2 * h + a), P * (2 * h + a + 1))
+            nc.tensor.matmul_mx(
+                out=y_bank[n, h][:, CHUNK * a : CHUNK * (a + 1)],
+                lhsT=kern_q[g, gi][0][:, cols].bitcast(FP8X4),
+                lhsT_scale=kern_q[g, gi][1][:, cols],
+                rhs=dc_q[GROUPS * c + g][0][:].bitcast(FP8X4),
+                rhs_scale=dc_q[GROUPS * c + g][1][:],
+                start=(g == 0), stop=(g == GROUPS - 1),
+            )
+
+        def open_bank(n, h):
+            y_bank[n, h] = new_bank("y_bank%d_%d" % (n, h))
+            for g in range(GROUPS - 1):
+                y_pass(n, h, 0, g)
+
         def new_gap(n):
             c, gi = divmod(n, GROUPS)
-            y_sb[n] = flow.tile([P, 4, CHUNK], F32, name="y%d" % n, tag="y", bufs=3)
+            y_sb[n] = flow.tile([P, 4, CHUNK], F32, name="y%d" % n, tag="big", bufs=BIG)
+            at = CHUNK * (c % 2)
             for h in range(2):
-                bank = psum.tile([P, PASS], F32, name="y_bank%d_%d" % (n, h), tag="second", bufs=2)
-                for a in range(2):
-                    cols = slice(P * (2 * h + a), P * (2 * h + a + 1))
-                    for g in range(GROUPS):
-                        nc.tensor.matmul_mx(
-                            out=bank[:, CHUNK * a : CHUNK * (a + 1)],
-                            lhsT=kern_q[g, gi][0][:, cols].bitcast(FP8X4),
-                            lhsT_scale=kern_q[g, gi][1][:, cols],
-                            rhs=dc_q[GROUPS * c + g][0][:].bitcast(FP8X4),
-                            rhs_scale=dc_q[GROUPS * c + g][1][:],
-                            start=(g == 0), stop=(g == GROUPS - 1),
-                        )
+                if (n, h) not in y_bank:
+                    open_bank(n, h)
+                y_pass(n, h, 0, GROUPS - 1)
+                for g in range(GROUPS):
+                    y_pass(n, h, 1, g)
                 nc.vector.tensor_tensor(
                     out=y_sb[n][:, 2 * h : 2 * h + 2, :],
-                    in0=bank[:].rearrange("p (a m) -> p a m", a=2),
-                    in1=src_sb[n][:, 2 * h : 2 * h + 2, :],
+                    in0=y_bank[n, h][:].rearrange("p (a m) -> p a m", a=2),
+                    in1=src_sb[gi, c // 2][:, 2 * h : 2 * h + 2, at : at + CHUNK],
                     op=ALU.add,
                 )
             nc.sync.dma_start(
@@ -268,8 +303,8 @@ def tile_bcs_gap_sweep_k4_kernel(
             )
 
         def round_y(n):
-            y_bf[n] = flow.tile([P, 4 * CHUNK], BF16, name="y_bf%d" % n, tag="y_bf", bufs=2, align_bytes=64)
-            nc.scalar.copy(
+            y_bf[n] = flow.tile([P, 4 * CHUNK], BF16, name="y_bf%d" % n, tag="y_bf", bufs=3, align_bytes=64)
+            (nc.vector.tensor_copy if n >= UNITS - LASTV else nc.scalar.copy)(
                 out=y_bf[n][:].rearrange("p (c i t) -> p c t i", i=2, t=4),
                 in_=y_sb[n][:].rearrange("p t (c i) -> p c t i", i=2),
             )
@@ -277,7 +312,7 @@ def tile_bcs_gap_sweep_k4_kernel(
         def quantise_y(n):
             c, gi = divmod(n, GROUPS)
             cols = slice(CHUNK * c, CHUNK * (c + 1))
-            codes = flow.tile([P, CHUNK], U32, name="y_codes%d" % n, tag="y_codes", bufs=3, align_bytes=64)
+            codes = flow.tile([P, CHUNK], U32, name="y_codes%d" % n, tag="y_codes", bufs=6, align_bytes=64)
             scales = y_scale_first[:, cols] if gi == 0 else y_scale_rest[4 * (gi - 1) :, cols]
             nc.vector.quantize_mx(out=codes[:].bitcast(FP8X4), scales=scales, in_=y_bf[n][:])
             nc.sync.dma_start(
@@ -285,7 +320,7 @@ def tile_bcs_gap_sweep_k4_kernel(
             )
             if c == CHUNKS - 1 and gi == 0:
                 for q in range(4):
-                    nc.sync.dma_start(
+                    nc.gpsimd.dma_start(
                         out=out_2[0, 4 * q : 4 * q + 4, :].bitcast(I32),
                         in_=y_scale_first[32 * q : 32 * q + 4, :].bitcast(I32),
                     )
@@ -299,6 +334,7 @@ def tile_bcs_gap_sweep_k4_kernel(
         c_q = planes("coef", SAMPLES)
 
         def sort_coefficients():
+            nc.vector.tensor_copy(out=beta[:], in_=beta_raw[:].rearrange("q c e -> q (c e)"))
             nc.vector.tensor_copy(
                 out=c_q[0][:].bitcast(I32).rearrange("p (c e a b) -> p c a e b", c=CHUNKS, e=2, b=4),
                 in_=c_raw[:].bitcast(I32).rearrange("p (c a b e) -> p c a e b", c=CHUNKS, e=2, b=4),
@@ -308,107 +344,147 @@ def tile_bcs_gap_sweep_k4_kernel(
                 in_=c_scale_raw[:].rearrange("p (c a b e) -> p c a e b", c=CHUNKS, e=2, b=16),
             )
 
-        kern_done = []
-        kern_total = 12 * GROUPS
+        kern_done, kern_quantised = [], []
 
-        def kern_banks(count):
-            for n in range(len(kern_done), min(len(kern_done) + count, kern_total)):
+        def kern_up_to(count):
+            for n in range(len(kern_done), min(count, 12 * GROUPS)):
                 kern_bank(n)
                 kern_done.append(n)
 
-        kern_quantised = []
-
-        def kern_quantise_ready(lag):
-            for q in range(len(kern_quantised), (len(kern_done) - lag) // 4):
+        def quantise_finished_kern():
+            for q in range(len(kern_quantised), max(len(kern_done) - 1, 0) // 4 if len(kern_done) < 36 else 9):
                 quantise_kern(q)
                 kern_quantised.append(q)
 
-        order = [GROUPS * (2 * h + cc) + g for h in range(2) for g in range(GROUPS) for cc in range(2)]
-        with tc.manual_schedule(engines={mybir.EngineType.Activation, mybir.EngineType.SP}):
-            load_right(0)
-            load_energy(0, 0)
-            load_left(0)
-            nc.sync.dma_start(out=meas[:], in_=measure.rearrange("(g p t) -> p g t", p=P, t=4))
-            load_right(1)
-            load_energy(1, 0)
-            load_right(2)
-            load_energy(2, 0)
-            load_energy(0, 1)
-            interleave_right(0)
-            turn_energy(order[0], "a")
-            for step, n in enumerate(order):
-                inverse_root(n)
-                if step == 0:
-                    turn_left(0)
-                if step + 1 < UNITS:
-                    turn_energy(order[step + 1], "a")
-                if step == 0:
-                    interleave_right(1)
-                    quantise_right(0)
-                    load_left(1)
-                    load_energy(1, 1)
-                    load_energy(2, 1)
-                    quantise_left(0)
-                if step == 1:
-                    interleave_right(2)
-                    quantise_right(1)
-                    load_left(2)
-                    nc.sync.dma_start(out=beta_raw[:], in_=half_beta.rearrange("(c q e) -> q c e", q=P, e=2))
-                    nc.sync.dma_start(out=c_raw[:].bitcast(I32), in_=c_words[0].rearrange("p n t -> p (n t)").bitcast(I32))
-                    for q in range(4):
-                        nc.sync.dma_start(
-                            out=c_scale_raw[32 * q : 32 * q + 4, :].bitcast(I32),
-                            in_=c_scales[0, 4 * q : 4 * q + 4, :].bitcast(I32),
-                        )
-                    for q in range(4):
-                        nc.sync.dma_start(
-                            out=phi_scale[32 * q : 32 * q + 4, :].bitcast(I32),
-                            in_=phi_scales[0, 4 * q : 4 * q + 4, :].bitcast(I32),
-                        )
-                    nc.sync.dma_start(out=phi[:].bitcast(I32), in_=phi_words[0].bitcast(I32))
-                if step >= KERN_START:
-                    kern_banks(KERN_EARLY)
-                if step == KERN_START:
-                    quantise_right(2)
-                if step == 6:
-                    turn_left(1)
-                if step == 7:
-                    quantise_left(1)
-                if step == 9:
-                    turn_left(2)
-                if step == 10:
-                    quantise_left(2)
-                kern_quantise_ready(1)
-            nc.scalar.copy(out=beta[:], in_=beta_raw[:].rearrange("q c e -> q (c e)"))
-            sort_coefficients()
-            for n in range(4):
-                load_source(n)
+        def load_small():
+            nc.sync.dma_start(out=beta_raw[:], in_=half_beta.rearrange("(c q e) -> q c e", q=P, e=2))
+            nc.sync.dma_start(out=c_raw[:].bitcast(I32), in_=c_words[0].rearrange("p n t -> p (n t)").bitcast(I32))
+            for q in range(4):
+                nc.sync.dma_start(
+                    out=c_scale_raw[32 * q : 32 * q + 4, :].bitcast(I32),
+                    in_=c_scales[0, 4 * q : 4 * q + 4, :].bitcast(I32),
+                )
+            for q in range(4):
+                nc.sync.dma_start(
+                    out=phi_scale[32 * q : 32 * q + 4, :].bitcast(I32),
+                    in_=phi_scales[0, 4 * q : 4 * q + 4, :].bitcast(I32),
+                )
+            nc.sync.dma_start(out=phi[:].bitcast(I32), in_=phi_words[0].bitcast(I32))
 
-        for n in range(SQ_EARLY):
-            square(n)
+        for w in LOADS.split():
+            if w[0] == "R":
+                load_right(int(w[1]))
+            if w[0] == "L":
+                load_left(int(w[1]))
+            if w[0] == "E":
+                load_energy(int(w[1]), int(w[2]))
+            if w[0] == "m":
+                nc.sync.dma_start(out=meas[:], in_=measure.rearrange("(g p t) -> p g t", p=P, t=4))
+            if w[0] == "s":
+                load_small()
+
+        order = [GROUPS * (2 * h + cc) + g for h in range(2) for g in range(GROUPS) for cc in range(2)]
+        early = int(KERN_EARLY * (UNITS - KERN_START))
+        steps = UNITS + 8
+        kern_count = [min(36, early + JUMP + int(KERN_LATE * (s + 1))) for s in range(steps)]
+        plan, placed = [], []
+        for s in range(steps):
+            ready = [
+                n for n in range(UNITS)
+                if n not in placed and s >= (3 * (n // 3) + Y_LAG if n < 9 else UNITS + 2)
+                and (early if s == 0 else kern_count[s - 1]) >= min(36, 12 * (n % 3 + 1) + 1)
+            ]
+            now = ready[: (1 if s < Y2 else 2)] if s < UNITS + 1 else ready[:1] if s > UNITS + 1 else [n for n in ready if n < 9]
+            plan.append(now)
+            placed.extend(now)
+        assert len(placed) == UNITS
+        interleave_right(0)
+        for step, n in enumerate(order):
+            if step == L0:
+                turn_left(0)
+            turn_energy(n, "a")
+            inverse_root(n)
+            if step == 0:
+                quantise_right(0)
+                if R1 == 0:
+                    interleave_right(1)
+            if step == L0:
+                quantise_left(0)
+            if step == 0 and R1 == 0:
+                pass
+            elif step == R1:
+                interleave_right(1)
+            if step == L1:
+                turn_left(1)
+            if step == L2:
+                turn_left(2)
+            kern_up_to(int(KERN_EARLY * (step + 1 - KERN_START)))
+            if step == R1 + 1:
+                quantise_right(1)
+            if step == R2:
+                interleave_right(2)
+            if step == R2 + 1:
+                quantise_right(2)
+            if step == L1 + 1:
+                quantise_left(1)
+            if step == L2 + 1:
+                quantise_left(2)
+            quantise_finished_kern()
+            if step == CSORT:
+                sort_coefficients()
+        squared = []
+
+        def squares_up_to(count):
+            for n in range(len(squared), min(count, UNITS)):
+                square(n)
+                squared.append(n)
+
         turn_energy(0, "b")
-        for step in range(UNITS + Y_LAG + 2):
-            if step < UNITS:
-                tanh(step)
+        tanh(0)
+        squares_up_to(1)
+        added, rounded, quantised = [], [], []
+        for step in range(steps):
             if step + 1 < UNITS:
                 turn_energy(step + 1, "b")
             if 0 <= step - 2 < UNITS:
                 turn_back(step - 2)
-            if 0 <= step - 1 < UNITS:
-                weighted_gap(step - 1)
+            if step == L2 - UNITS:
+                turn_left(2)
+            if step + 1 < UNITS:
+                tanh(step + 1)
+            if 0 <= step - 2 < UNITS:
+                copy_back(step - 2)
             if step < UNITS:
                 weight(step)
-            if step + SQ_EARLY < UNITS:
-                square(step + SQ_EARLY)
-            if 0 <= step - Y_LAG < UNITS:
-                new_gap(step - Y_LAG)
-                if step - Y_LAG + 4 < UNITS:
-                    load_source(step - Y_LAG + 4)
-            kern_banks(KERN_LATE)
+            if 0 <= step - 1 < UNITS:
+                weighted_gap(step - 1)
+            squares_up_to(1 + int(SQ_RATE * (step + 1)))
+            before = len(added)
+            for n in plan[step]:
+                new_gap(n)
+                added.append(n)
+            if step == UNITS + 1:
+                for n in range(UNITS - GROUPS, UNITS - GROUPS + OPEN):
+                    for h in range(2):
+                        open_bank(n, h)
+            if step == L2 - UNITS:
+                for h in range(2):
+                    for gi in range(GROUPS):
+                        load_source(gi, h)
+            kern_up_to(kern_count[step])
+            if step < UNITS:
+                weight_rest(step)
+            if step == L2 - UNITS:
+                quantise_left(2)
+            quantise_finished_kern()
+            for n in rounded[len(quantised) :]:
+                quantise_y(n)
+                quantised.append(n)
             if 0 <= step - 2 < UNITS:
                 quantise_gap(step - 2)
-            if 0 <= step - Y_LAG - 1 < UNITS:
-                quantise_y(step - Y_LAG - 1)
-            kern_quantise_ready(0)
-            if 0 <= step - Y_LAG < UNITS:
-                round_y(step - Y_LAG)
+            for n in added[len(rounded) : min(int(R_RATE * max(step - R_LAG + 1, 0)), before + R_OFF)]:
+                round_y(n)
+                rounded.append(n)
+        for n in rounded[len(quantised) :]:
+            quantise_y(n)
+        assert len(rounded) == UNITS

@@ -17,37 +17,24 @@ MOMENTA, SAMPLES, RANK, BASIS = 1536, 1024, 512, 512
 FLOPS = 2 * MOMENTA * (MOMENTA * RANK + BASIS * SAMPLES + MOMENTA * SAMPLES)
 
 P = 128
-PASS = 512
-GROUPS = MOMENTA // PASS
-CHUNK = 256
+SLOTS = 4
+GROUP = P * SLOTS
+GROUPS = MOMENTA // GROUP
+CHUNK = 2 * P
 CHUNKS = SAMPLES // CHUNK
+HALF = SAMPLES // 2
 UNITS = CHUNKS * GROUPS
+KERN_BANKS = GROUPS * GROUPS * SLOTS
 
-KERN_START = 1
-KERN_EARLY = 1.6
-KERN_LATE = 1.8
-Y_LAG = 5
-SQ_EARLY = 2
-BIG = 13
-LEFT_S = (0, 1, 2,)
-L1 = 5
-L2 = 12
-CSORT = 9
-R_LAG = 7
-THB = 2
-JUMP = 3
-LASTV = 1
-R2 = 2
-OPEN = 0
-LOADS = "R0 L0 E00 m R1 E10 R2 E20 L1 E01 E11 E21 s L2"
-L0 = 0
-R1 = 1
-SQ_RATE = 1
-Y2 = 11
-G_COLS = 896
-RIGHT_S = ()
-R_RATE = 1.3
-R_OFF = 1
+KERN_FIRST_STEP = 2
+KERN_EARLY = 1.8
+KERN_BRIDGE = 3
+KERN_LATE = 2.2
+SQUARES = 1.5
+SORT_STEP = 9
+Y_LAG = GROUPS + 2
+TANH_BUFS = 3
+WIDE_BUFS = 6
 
 
 def tile_bcs_gap_sweep_k4_kernel(
@@ -57,17 +44,49 @@ def tile_bcs_gap_sweep_k4_kernel(
     nc = tc.nc
     with ExitStack() as ctx:
         keep = ctx.enter_context(tc.tile_pool(name="keep", bufs=1))
-        flow = ctx.enter_context(tc.tile_pool(name="flow", bufs=2))
+        flow = ctx.enter_context(tc.tile_pool(name="flow", bufs=1))
         psum = ctx.enter_context(tc.psum_pool(name="psum", bufs=1))
         ctx.enter_context(tc.manual_schedule())
 
-        def planes(name, width):
+        def new_bank(name):
+            return psum.tile([P, GROUP], F32, name=name, tag="ring", bufs=8)
+
+        def new_operand(name, width):
             codes = keep.tile([P, width], U32, name=name + "_codes", align_bytes=64)
             scales = keep.tile([P, width], U8, name=name + "_scales", align_bytes=64)
             return codes, scales
 
-        def new_bank(name):
-            return psum.tile([P, PASS], F32, name=name, tag="ring", bufs=8)
+        def raw_tile(name):
+            return flow.tile([P, SLOTS, GROUP], BF16, name=name, tag="raw", bufs=2 * GROUPS)
+
+        def wide_tile(name):
+            return flow.tile([P, SLOTS * GROUP], BF16, name=name, tag="wide", bufs=WIDE_BUFS, align_bytes=64)
+
+        def unit_tile(name, shape):
+            return flow.tile(shape, F32, name=name, tag="unit", bufs=UNITS + 1)
+
+        def turn_tile(name, dtype):
+            return flow.tile([P, 2 * GROUP], dtype, name=name, tag="turn", bufs=3, align_bytes=64)
+
+        def rows(ap, g):
+            return ap[GROUP * g : GROUP * (g + 1), :].rearrange("(p t) c -> p t c", t=SLOTS)
+
+        def part(i, size):
+            return slice(size * i, size * (i + 1))
+
+        def quantise(operand, values):
+            nc.vector.quantize_mx(out=operand[0][:].bitcast(FP8X4), scales=operand[1][:], in_=values[:])
+
+        def multiply(out, stationary, stationary_cols, moving, moving_cols, start, stop):
+            nc.tensor.matmul_mx(
+                out=out,
+                lhsT=stationary[0][:, stationary_cols].bitcast(FP8X4),
+                lhsT_scale=stationary[1][:, stationary_cols],
+                rhs=moving[0][:, moving_cols].bitcast(FP8X4),
+                rhs_scale=moving[1][:, moving_cols],
+                start=start,
+                stop=stop,
+            )
 
         ident = keep.tile([P, P], F32, name="ident")
         make_identity(nc, ident[:])
@@ -76,415 +95,335 @@ def tile_bcs_gap_sweep_k4_kernel(
         nc.gpsimd.memset(phi_scale[:].bitcast(I32), 0)
         nc.gpsimd.memset(c_scale_raw[:].bitcast(I32), 0)
 
-        right_raw, left_raw, e_sb, src_sb = {}, {}, {}, {}
-
-        def load_right(g):
-            right_raw[g] = flow.tile([P, 4, PASS], BF16, name="right_raw%d" % g, tag="raw", bufs=6)
-            nc.sync.dma_start(
-                out=right_raw[g][:],
-                in_=pair_right[:, PASS * g : PASS * (g + 1)].rearrange("(p j) c -> p j c", j=4),
-            )
-
-        def load_left(gi):
-            left_raw[gi] = flow.tile([P, 4, RANK], BF16, name="left_raw%d" % gi, tag="raw", bufs=6)
-            nc.sync.dma_start(
-                out=left_raw[gi][:],
-                in_=pair_left[PASS * gi : PASS * (gi + 1), :].rearrange("(p t) k -> p t k", t=4),
-            )
-
-        def load_energy(g, h):
-            e_sb[g, h] = keep.tile([P, 4, PASS], BF16, name="energy%d_%d" % (g, h))
-            nc.sync.dma_start(
-                out=e_sb[g, h][:],
-                in_=energy[PASS * g : PASS * (g + 1), PASS * h : PASS * (h + 1)].rearrange("(p t) m -> p t m", t=4),
-            )
-
-        def load_source(gi, h):
-            src_sb[gi, h] = flow.tile([P, 4, PASS], BF16, name="source%d_%d" % (gi, h), tag="raw", bufs=6)
-            nc.sync.dma_start(
-                out=src_sb[gi, h][:],
-                in_=source[PASS * gi : PASS * (gi + 1), PASS * h : PASS * (h + 1)].rearrange("(p t) m -> p t m", t=4),
-            )
-
-        meas = keep.tile([P, GROUPS, 4], BF16, name="meas")
+        meas = keep.tile([P, GROUPS, SLOTS], BF16, name="meas")
         beta_raw = keep.tile([P, CHUNKS, 2], BF16, name="beta_raw")
         beta = keep.tile([P, CHUNKS * 2], F32, name="beta")
         phi = keep.tile([P, 2 * MOMENTA], U8, name="phi", align_bytes=64)
         c_raw = keep.tile([P, SAMPLES], U32, name="c_raw", align_bytes=64)
-
-        right_q, left_q, kern_q, dc_q = {}, {}, {}, {}
-        grouped = {}
-
-        def quantise(src, dst):
-            nc.vector.quantize_mx(out=dst[0][:].bitcast(FP8X4), scales=dst[1][:], in_=src[:])
-
-        def wide_tile(name):
-            return flow.tile([P, 4 * PASS], BF16, name=name, tag="wide", bufs=4, align_bytes=64)
-
-        def interleave_right(g):
-            grouped["r", g] = wide_tile("right_wide%d" % g)
-            (nc.scalar.copy if g in RIGHT_S else nc.vector.tensor_copy)(
-                out=grouped["r", g][:].rearrange("p (t a b j) -> p a t b j", t=4, b=2, j=4),
-                in_=right_raw[g][:].rearrange("p j (a b t) -> p a t b j", b=2, t=4),
-            )
-
-        def quantise_right(g):
-            right_q[g] = planes("right%d" % g, PASS)
-            quantise(grouped["r", g], right_q[g])
-
-        def turn_left(gi):
-            grouped["l", gi] = wide_tile("left_wide%d" % gi)
-            words = left_raw[gi][:].rearrange("p t k -> p (t k)").bitcast(F32)
-            wide_words = grouped["l", gi][:].bitcast(F32)
-            for h in range(2):
-                bank = new_bank("left_bank%d_%d" % (gi, h))
-                for a in range(4):
-                    t, u = 2 * h + a // 2, a % 2
-                    nc.tensor.transpose(bank[:, P * a : P * (a + 1)], words[:, 256 * t + u : 256 * (t + 1) : 2], ident[:])
-                (nc.scalar.copy if gi in LEFT_S else nc.vector.tensor_copy)(
-                    out=wide_words[:, PASS * h : PASS * (h + 1)].rearrange("p (t i u) -> p t i u", t=2, u=2),
-                    in_=bank[:].rearrange("p (t u i) -> p t i u", t=2, u=2),
-                )
-
-        def quantise_left(gi):
-            left_q[gi] = planes("left%d" % gi, PASS)
-            quantise(grouped["l", gi], left_q[gi])
-
-        def kern_bank(n):
-            gi, g, s = n // 12, n // 4 % 3, n % 4
-            if s == 0:
-                grouped["k", g, gi] = wide_tile("kern_wide%d_%d" % (g, gi))
-            bank = new_bank("kern_bank%d" % n)
-            cols = slice(P * s, P * (s + 1))
-            for t in range(4):
-                nc.tensor.matmul_mx(
-                    out=bank[:, P * t : P * (t + 1)],
-                    lhsT=right_q[g][0][:, P * t : P * (t + 1)].bitcast(FP8X4),
-                    lhsT_scale=right_q[g][1][:, P * t : P * (t + 1)],
-                    rhs=left_q[gi][0][:, cols].bitcast(FP8X4),
-                    rhs_scale=left_q[gi][1][:, cols],
-                    start=True, stop=True,
-                )
-            nc.vector.tensor_tensor(
-                out=grouped["k", g, gi][:, PASS * s : PASS * (s + 1)].rearrange("p (i t) -> p i t", t=4),
-                in0=bank[:].rearrange("p (t i) -> p i t", t=4),
-                in1=meas[:, g, :].unsqueeze(1).to_broadcast([P, P, 4]),
-                op=ALU.mult,
-            )
-
-        def quantise_kern(q):
-            gi, g = divmod(q, GROUPS)
-            kern_q[g, gi] = planes("kern%d_%d" % (g, gi), PASS)
-            quantise(grouped["k", g, gi], kern_q[g, gi])
-
-        back = {}
-        e_bank, inv, th, chi, delta, dct, dcw, y_bank, y_sb, y_bf = {}, {}, {}, {}, {}, {}, {}, {}, {}, {}
-
-        def turn_energy(n, use):
-            c, g = divmod(n, GROUPS)
-            words = e_sb[g, c // 2][:].rearrange("p t m -> p (t m)").bitcast(F32)
-            bank = new_bank("e_bank%s%d" % (use, n))
-            for t in range(4):
-                at = 256 * t + P * (c % 2)
-                nc.tensor.transpose(bank[:, P * t : P * (t + 1)], words[:, at : at + P], ident[:])
-            e_bank[n] = bank[:].bitcast(BF16).rearrange("q (u b p e) -> q e u p b", u=2, b=2, e=2)
-
-        def in_word_order(ap):
-            return ap.rearrange("q (u p b) -> q u p b", u=2, b=2)
-
-        def inverse_root(n):
-            inv[n] = flow.tile([P, 2 * PASS], F32, name="inv%d" % n, tag="big", bufs=BIG)
-            for e in range(2):
-                nc.scalar.activation(
-                    out=in_word_order(inv[n][:, PASS * e : PASS * (e + 1)]), in_=e_bank[n][:, e, :, :, :],
-                    func=ACT.Abs_reciprocal_sqrt, scale=2.0,
-                )
-
-        def square(n):
-            nc.scalar.activation(out=inv[n][:], in_=inv[n][:], func=ACT.Square)
-
-        def tanh(n):
-            c = n // GROUPS
-            th[n] = flow.tile([P, 2 * PASS], F32, name="tanh%d" % n, tag="tanh", bufs=THB)
-            for e in range(2):
-                nc.scalar.activation(
-                    out=in_word_order(th[n][:, PASS * e : PASS * (e + 1)]), in_=e_bank[n][:, e, :, :, :], func=ACT.Tanh,
-                    scale=beta[:, 2 * c + e : 2 * c + e + 1],
-                )
-
-        def weight(n):
-            chi[n] = flow.tile([P, 2 * PASS], F32, name="chi%d" % n, tag="turns", bufs=3, align_bytes=64)
-            if G_COLS > 0:
-                nc.gpsimd.tensor_tensor(out=chi[n][:, :G_COLS], in0=th[n][:, :G_COLS], in1=inv[n][:, :G_COLS], op=ALU.mult)
-
-        def weight_rest(n):
-            if G_COLS < 1024:
-                nc.vector.tensor_tensor(out=chi[n][:, G_COLS:], in0=th[n][:, G_COLS:], in1=inv[n][:, G_COLS:], op=ALU.mult)
-
-        def weighted_gap(n):
-            c, g = divmod(n, GROUPS)
-            dct[n] = flow.tile([P, 2 * PASS], BF16, name="dct%d" % n, tag="dct", bufs=2)
-            for e in range(2):
-                bank = new_bank("delta_bank%d_%d" % (n, e))
-                cols = slice(CHUNK * c + P * e, CHUNK * c + P * (e + 1))
-                nc.tensor.matmul_mx(
-                    out=bank[:],
-                    lhsT=c_q[0][:, cols].bitcast(FP8X4),
-                    lhsT_scale=c_q[1][:, cols],
-                    rhs=phi[:, 2 * PASS * g : 2 * PASS * (g + 1)].bitcast(FP4X4),
-                    rhs_scale=phi_scale[:, PASS * g : PASS * (g + 1)],
-                    start=True, stop=True,
-                )
-                nc.vector.tensor_tensor(
-                    out=in_word_order(dct[n][:, PASS * e : PASS * (e + 1)]),
-                    in0=bank[:].rearrange("q (p u b) -> q u p b", u=2, b=2),
-                    in1=in_word_order(chi[n][:, PASS * e : PASS * (e + 1)]),
-                    op=ALU.mult,
-                )
-
-        def turn_back(n):
-            words = dct[n][:].bitcast(F32)
-            bank = new_bank("back_bank%d" % n)
-            for a in range(4):
-                nc.tensor.transpose(bank[:, P * a : P * (a + 1)], words[:, P * a : P * (a + 1)], ident[:])
-            back[n] = bank
-
-        def copy_back(n):
-            bank = back[n]
-            dcw[n] = flow.tile([P, 4 * CHUNK], BF16, name="dcw%d" % n, tag="turns", bufs=3, align_bytes=64)
-            nc.scalar.copy(
-                out=dcw[n][:].bitcast(F32).rearrange("p (q a) -> p q a", a=4),
-                in_=bank[:].rearrange("p (a q) -> p q a", a=4),
-            )
-
-        def quantise_gap(n):
-            dc_q[n] = planes("dc%d" % n, CHUNK)
-            quantise(dcw[n], dc_q[n])
-
+        coef = new_operand("coef", SAMPLES)
         y_scale_first = keep.tile([P, SAMPLES], U8, name="y_scale_first", align_bytes=64)
         y_scale_rest = keep.tile([P, SAMPLES], U8, name="y_scale_rest", align_bytes=64)
 
-        def y_pass(n, h, a, g):
-            c, gi = divmod(n, GROUPS)
-            cols = slice(P * (2 * h + a), P * (2 * h + a + 1))
-            nc.tensor.matmul_mx(
-                out=y_bank[n, h][:, CHUNK * a : CHUNK * (a + 1)],
-                lhsT=kern_q[g, gi][0][:, cols].bitcast(FP8X4),
-                lhsT_scale=kern_q[g, gi][1][:, cols],
-                rhs=dc_q[GROUPS * c + g][0][:].bitcast(FP8X4),
-                rhs_scale=dc_q[GROUPS * c + g][1][:],
-                start=(g == 0), stop=(g == GROUPS - 1),
-            )
+        right_raw, right_wide, right_q = {}, {}, {}
+        left_raw, left_wide, left_q = {}, {}, {}
+        kern_wide, kern_q = {}, {}
+        energy_sb, energy_t, inverse, tanh_sb, chi = {}, {}, {}, {}, {}
+        gap_t, gap_bank, gap_wide, gap_q = {}, {}, {}, {}
+        source_sb, y_bank, y_sb, y_wide = {}, {}, {}, {}
 
-        def open_bank(n, h):
-            y_bank[n, h] = new_bank("y_bank%d_%d" % (n, h))
-            for g in range(GROUPS - 1):
-                y_pass(n, h, 0, g)
 
-        def new_gap(n):
-            c, gi = divmod(n, GROUPS)
-            y_sb[n] = flow.tile([P, 4, CHUNK], F32, name="y%d" % n, tag="big", bufs=BIG)
-            at = CHUNK * (c % 2)
-            for h in range(2):
-                if (n, h) not in y_bank:
-                    open_bank(n, h)
-                y_pass(n, h, 0, GROUPS - 1)
-                for g in range(GROUPS):
-                    y_pass(n, h, 1, g)
-                nc.vector.tensor_tensor(
-                    out=y_sb[n][:, 2 * h : 2 * h + 2, :],
-                    in0=y_bank[n, h][:].rearrange("p (a m) -> p a m", a=2),
-                    in1=src_sb[gi, c // 2][:, 2 * h : 2 * h + 2, at : at + CHUNK],
-                    op=ALU.add,
+        def load_right(g):
+            right_raw[g] = raw_tile("right_raw%d" % g)
+            nc.sync.dma_start(out=right_raw[g][:], in_=rows(pair_right[:, part(g, GROUP)], 0))
+
+        def load_left(g):
+            left_raw[g] = raw_tile("left_raw%d" % g)
+            nc.sync.dma_start(out=left_raw[g][:], in_=rows(pair_left, g))
+
+        def load_energy(g, h):
+            energy_sb[g, h] = keep.tile([P, SLOTS, HALF], BF16, name="energy%d_%d" % (g, h))
+            nc.sync.dma_start(out=energy_sb[g, h][:], in_=rows(energy[:, part(h, HALF)], g))
+
+        def load_source(g, h):
+            source_sb[g, h] = raw_tile("source%d_%d" % (g, h))
+            nc.sync.dma_start(out=source_sb[g, h][:], in_=rows(source[:, part(h, HALF)], g))
+
+        def load_scale_rows(tile, scales):
+            for quad in range(4):
+                nc.sync.dma_start(
+                    out=tile[32 * quad : 32 * quad + 4, :].bitcast(I32), in_=scales[0, part(quad, 4), :].bitcast(I32)
                 )
-            nc.sync.dma_start(
-                out=out_0[PASS * gi : PASS * (gi + 1), CHUNK * c : CHUNK * (c + 1)].rearrange("(p t) m -> p t m", t=4),
-                in_=y_sb[n][:],
+
+
+        def interleave_right(g):
+            right_wide[g] = wide_tile("right_wide%d" % g)
+            nc.vector.tensor_copy(
+                out=right_wide[g][:].rearrange("p (t a b s) -> p a t b s", t=SLOTS, b=2, s=SLOTS),
+                in_=right_raw[g][:].rearrange("p s (a b t) -> p a t b s", b=2, t=SLOTS),
             )
 
-        def round_y(n):
-            y_bf[n] = flow.tile([P, 4 * CHUNK], BF16, name="y_bf%d" % n, tag="y_bf", bufs=3, align_bytes=64)
-            (nc.vector.tensor_copy if n >= UNITS - LASTV else nc.scalar.copy)(
-                out=y_bf[n][:].rearrange("p (c i t) -> p c t i", i=2, t=4),
-                in_=y_sb[n][:].rearrange("p t (c i) -> p c t i", i=2),
-            )
+        def quantise_right(g):
+            right_q[g] = new_operand("right%d" % g, GROUP)
+            quantise(right_q[g], right_wide[g])
 
-        def quantise_y(n):
-            c, gi = divmod(n, GROUPS)
-            cols = slice(CHUNK * c, CHUNK * (c + 1))
-            codes = flow.tile([P, CHUNK], U32, name="y_codes%d" % n, tag="y_codes", bufs=6, align_bytes=64)
-            scales = y_scale_first[:, cols] if gi == 0 else y_scale_rest[4 * (gi - 1) :, cols]
-            nc.vector.quantize_mx(out=codes[:].bitcast(FP8X4), scales=scales, in_=y_bf[n][:])
-            nc.sync.dma_start(
-                out=out_1[gi].rearrange("p m t -> p (m t)").bitcast(I32)[:, cols], in_=codes[:].bitcast(I32)
-            )
-            if c == CHUNKS - 1 and gi == 0:
-                for q in range(4):
-                    nc.gpsimd.dma_start(
-                        out=out_2[0, 4 * q : 4 * q + 4, :].bitcast(I32),
-                        in_=y_scale_first[32 * q : 32 * q + 4, :].bitcast(I32),
+        def turn_left(g):
+            left_wide[g] = wide_tile("left_wide%d" % g)
+            words = left_raw[g][:].rearrange("p t r -> p (t r)").bitcast(F32)
+            for pair in range(2):
+                bank = new_bank("left_bank%d_%d" % (g, pair))
+                for a in range(4):
+                    t, u = 2 * pair + a // 2, a % 2
+                    nc.tensor.transpose(
+                        bank[:, part(a, P)], words[:, RANK // 2 * t + u : RANK // 2 * (t + 1) : 2], ident[:]
                     )
-            if c == CHUNKS - 1 and gi == GROUPS - 1:
-                for q in range(4):
-                    nc.sync.dma_start(
-                        out=out_2[1:, 4 * q : 4 * q + 4, :].bitcast(I32),
-                        in_=y_scale_rest[32 * q : 32 * q + 8, :].bitcast(I32),
-                    )
+                nc.scalar.copy(
+                    out=left_wide[g][:].bitcast(F32)[:, part(pair, GROUP)].rearrange("p (t i u) -> p t i u", t=2, u=2),
+                    in_=bank[:].rearrange("p (t u i) -> p t i u", t=2, u=2),
+                )
 
-        c_q = planes("coef", SAMPLES)
+        def quantise_left(g):
+            left_q[g] = new_operand("left%d" % g, GROUP)
+            quantise(left_q[g], left_wide[g])
+
+        def kern_bank(b):
+            gi, gj, s = b // (GROUPS * SLOTS), b // SLOTS % GROUPS, b % SLOTS
+            if s == 0:
+                kern_wide[gj, gi] = wide_tile("kern_wide%d_%d" % (gj, gi))
+            bank = new_bank("kern_bank%d" % b)
+            for t in range(SLOTS):
+                multiply(bank[:, part(t, P)], right_q[gj], part(t, P), left_q[gi], part(s, P), True, True)
+            nc.vector.tensor_tensor(
+                out=kern_wide[gj, gi][:, part(s, GROUP)].rearrange("p (i t) -> p i t", t=SLOTS),
+                in0=bank[:].rearrange("p (t i) -> p i t", t=SLOTS),
+                in1=meas[:, gj, :].unsqueeze(1).to_broadcast([P, P, SLOTS]),
+                op=ALU.mult,
+            )
+
+        kern_made = []
+
+        def kern_up_to(count):
+            for b in range(len(kern_made), min(count, KERN_BANKS)):
+                kern_bank(b)
+                kern_made.append(b)
+
+        def quantise_kern():
+            made = len(kern_made)
+            for tile in range(len(kern_q), made // SLOTS if made == KERN_BANKS else max(made - 1, 0) // SLOTS):
+                gi, gj = divmod(tile, GROUPS)
+                kern_q[gj, gi] = new_operand("kern%d_%d" % (gj, gi), GROUP)
+                quantise(kern_q[gj, gi], kern_wide[gj, gi])
+
 
         def sort_coefficients():
             nc.vector.tensor_copy(out=beta[:], in_=beta_raw[:].rearrange("q c e -> q (c e)"))
             nc.vector.tensor_copy(
-                out=c_q[0][:].bitcast(I32).rearrange("p (c e a b) -> p c a e b", c=CHUNKS, e=2, b=4),
+                out=coef[0][:].bitcast(I32).rearrange("p (c e a b) -> p c a e b", c=CHUNKS, e=2, b=4),
                 in_=c_raw[:].bitcast(I32).rearrange("p (c a b e) -> p c a e b", c=CHUNKS, e=2, b=4),
             )
             nc.vector.tensor_copy(
-                out=c_q[1][:].rearrange("p (c e a b) -> p c a e b", c=CHUNKS, e=2, b=16),
+                out=coef[1][:].rearrange("p (c e a b) -> p c a e b", c=CHUNKS, e=2, b=16),
                 in_=c_scale_raw[:].rearrange("p (c a b e) -> p c a e b", c=CHUNKS, e=2, b=16),
             )
 
-        kern_done, kern_quantised = [], []
+        def in_word_order(ap):
+            return ap.rearrange("q (u p b) -> q u p b", u=2, b=2)
 
-        def kern_up_to(count):
-            for n in range(len(kern_done), min(count, 12 * GROUPS)):
-                kern_bank(n)
-                kern_done.append(n)
+        def turn_energy(n, phase):
+            c, g = divmod(n, GROUPS)
+            words = energy_sb[g, c // 2][:].rearrange("p t m -> p (t m)").bitcast(F32)
+            bank = new_bank("energy_bank%d_%d" % (phase, n))
+            for t in range(SLOTS):
+                nc.tensor.transpose(bank[:, part(t, P)], words[:, part(2 * t + c % 2, P)], ident[:])
+            energy_t[n] = bank[:].bitcast(BF16).rearrange("q (u b p e) -> q e u p b", u=2, b=2, e=2)
 
-        def quantise_finished_kern():
-            for q in range(len(kern_quantised), max(len(kern_done) - 1, 0) // 4 if len(kern_done) < 36 else 9):
-                quantise_kern(q)
-                kern_quantised.append(q)
-
-        def load_small():
-            nc.sync.dma_start(out=beta_raw[:], in_=half_beta.rearrange("(c q e) -> q c e", q=P, e=2))
-            nc.sync.dma_start(out=c_raw[:].bitcast(I32), in_=c_words[0].rearrange("p n t -> p (n t)").bitcast(I32))
-            for q in range(4):
-                nc.sync.dma_start(
-                    out=c_scale_raw[32 * q : 32 * q + 4, :].bitcast(I32),
-                    in_=c_scales[0, 4 * q : 4 * q + 4, :].bitcast(I32),
+        def inverse_root(n):
+            inverse[n] = unit_tile("inverse%d" % n, [P, 2 * GROUP])
+            for e in range(2):
+                nc.scalar.activation(
+                    out=in_word_order(inverse[n][:, part(e, GROUP)]),
+                    in_=energy_t[n][:, e, :, :, :],
+                    func=ACT.Abs_reciprocal_sqrt,
+                    scale=2.0,
                 )
-            for q in range(4):
-                nc.sync.dma_start(
-                    out=phi_scale[32 * q : 32 * q + 4, :].bitcast(I32),
-                    in_=phi_scales[0, 4 * q : 4 * q + 4, :].bitcast(I32),
-                )
-            nc.sync.dma_start(out=phi[:].bitcast(I32), in_=phi_words[0].bitcast(I32))
 
-        for w in LOADS.split():
-            if w[0] == "R":
-                load_right(int(w[1]))
-            if w[0] == "L":
-                load_left(int(w[1]))
-            if w[0] == "E":
-                load_energy(int(w[1]), int(w[2]))
-            if w[0] == "m":
-                nc.sync.dma_start(out=meas[:], in_=measure.rearrange("(g p t) -> p g t", p=P, t=4))
-            if w[0] == "s":
-                load_small()
-
-        order = [GROUPS * (2 * h + cc) + g for h in range(2) for g in range(GROUPS) for cc in range(2)]
-        early = int(KERN_EARLY * (UNITS - KERN_START))
-        steps = UNITS + 8
-        kern_count = [min(36, early + JUMP + int(KERN_LATE * (s + 1))) for s in range(steps)]
-        plan, placed = [], []
-        for s in range(steps):
-            ready = [
-                n for n in range(UNITS)
-                if n not in placed and s >= (3 * (n // 3) + Y_LAG if n < 9 else UNITS + 2)
-                and (early if s == 0 else kern_count[s - 1]) >= min(36, 12 * (n % 3 + 1) + 1)
-            ]
-            now = ready[: (1 if s < Y2 else 2)] if s < UNITS + 1 else ready[:1] if s > UNITS + 1 else [n for n in ready if n < 9]
-            plan.append(now)
-            placed.extend(now)
-        assert len(placed) == UNITS
-        interleave_right(0)
-        for step, n in enumerate(order):
-            if step == L0:
-                turn_left(0)
-            turn_energy(n, "a")
-            inverse_root(n)
-            if step == 0:
-                quantise_right(0)
-                if R1 == 0:
-                    interleave_right(1)
-            if step == L0:
-                quantise_left(0)
-            if step == 0 and R1 == 0:
-                pass
-            elif step == R1:
-                interleave_right(1)
-            if step == L1:
-                turn_left(1)
-            if step == L2:
-                turn_left(2)
-            kern_up_to(int(KERN_EARLY * (step + 1 - KERN_START)))
-            if step == R1 + 1:
-                quantise_right(1)
-            if step == R2:
-                interleave_right(2)
-            if step == R2 + 1:
-                quantise_right(2)
-            if step == L1 + 1:
-                quantise_left(1)
-            if step == L2 + 1:
-                quantise_left(2)
-            quantise_finished_kern()
-            if step == CSORT:
-                sort_coefficients()
         squared = []
 
         def squares_up_to(count):
             for n in range(len(squared), min(count, UNITS)):
-                square(n)
+                nc.scalar.activation(out=inverse[n][:], in_=inverse[n][:], func=ACT.Square)
                 squared.append(n)
 
-        turn_energy(0, "b")
+        def tanh(n):
+            tanh_sb[n] = flow.tile([P, 2 * GROUP], F32, name="tanh%d" % n, tag="tanh", bufs=TANH_BUFS)
+            for e in range(2):
+                nc.scalar.activation(
+                    out=in_word_order(tanh_sb[n][:, part(e, GROUP)]),
+                    in_=energy_t[n][:, e, :, :, :],
+                    func=ACT.Tanh,
+                    scale=beta[:, part(2 * (n // GROUPS) + e, 1)],
+                )
+
+        def pair_weight(n):
+            chi[n] = turn_tile("chi%d" % n, F32)
+            nc.gpsimd.tensor_tensor(out=chi[n][:], in0=tanh_sb[n][:], in1=inverse[n][:], op=ALU.mult)
+
+        def weighted_gap(n):
+            c, g = divmod(n, GROUPS)
+            gap_t[n] = flow.tile([P, 2 * GROUP], BF16, name="gap_t%d" % n, tag="gap_t", bufs=2)
+            for e in range(2):
+                bank = new_bank("delta_bank%d_%d" % (n, e))
+                nc.tensor.matmul_mx(
+                    out=bank[:],
+                    lhsT=coef[0][:, part(2 * c + e, P)].bitcast(FP8X4),
+                    lhsT_scale=coef[1][:, part(2 * c + e, P)],
+                    rhs=phi[:, part(g, 2 * GROUP)].bitcast(FP4X4),
+                    rhs_scale=phi_scale[:, part(g, GROUP)],
+                    start=True,
+                    stop=True,
+                )
+                nc.vector.tensor_tensor(
+                    out=in_word_order(gap_t[n][:, part(e, GROUP)]),
+                    in0=bank[:].rearrange("q (p u b) -> q u p b", u=2, b=2),
+                    in1=in_word_order(chi[n][:, part(e, GROUP)]),
+                    op=ALU.mult,
+                )
+
+        def turn_back(n):
+            gap_bank[n] = new_bank("gap_bank%d" % n)
+            for a in range(4):
+                nc.tensor.transpose(gap_bank[n][:, part(a, P)], gap_t[n][:].bitcast(F32)[:, part(a, P)], ident[:])
+
+        def copy_back(n):
+            gap_wide[n] = turn_tile("gap_wide%d" % n, BF16)
+            nc.scalar.copy(
+                out=gap_wide[n][:].bitcast(F32).rearrange("p (q a) -> p q a", a=4),
+                in_=gap_bank[n][:].rearrange("p (a q) -> p q a", a=4),
+            )
+
+        def quantise_gap(n):
+            gap_q[n] = new_operand("gap%d" % n, CHUNK)
+            quantise(gap_q[n], gap_wide[n])
+
+
+        def y_pass(n, t, gj):
+            c, gi = divmod(n, GROUPS)
+            multiply(
+                y_bank[n, t // 2][:, part(t % 2, CHUNK)], kern_q[gj, gi], part(t, P), gap_q[GROUPS * c + gj],
+                part(0, CHUNK), gj == 0, gj == GROUPS - 1,
+            )
+
+        def open_y_bank(n, pair):
+            y_bank[n, pair] = new_bank("y_bank%d_%d" % (n, pair))
+            for gj in range(GROUPS - 1):
+                y_pass(n, 2 * pair, gj)
+
+        def new_gap(n):
+            c, gi = divmod(n, GROUPS)
+            y_sb[n] = unit_tile("y%d" % n, [P, SLOTS, CHUNK])
+            for pair in range(2):
+                if (n, pair) not in y_bank:
+                    open_y_bank(n, pair)
+                y_pass(n, 2 * pair, GROUPS - 1)
+                for gj in range(GROUPS):
+                    y_pass(n, 2 * pair + 1, gj)
+                nc.vector.tensor_tensor(
+                    out=y_sb[n][:, part(pair, 2), :],
+                    in0=y_bank[n, pair][:].rearrange("p (t m) -> p t m", t=2),
+                    in1=source_sb[gi, c // 2][:, part(pair, 2), part(c % 2, CHUNK)],
+                    op=ALU.add,
+                )
+            nc.sync.dma_start(out=rows(out_0[:, part(c, CHUNK)], gi), in_=y_sb[n][:])
+
+        def round_y(n):
+            y_wide[n] = flow.tile([P, SLOTS * CHUNK], BF16, name="y_wide%d" % n, tag="y_wide", bufs=3, align_bytes=64)
+            copy = nc.vector.tensor_copy if n == UNITS - 1 else nc.scalar.copy
+            copy(
+                out=y_wide[n][:].rearrange("p (a b t) -> p a t b", b=2, t=SLOTS),
+                in_=y_sb[n][:].rearrange("p t (a b) -> p a t b", b=2),
+            )
+
+        def quantise_y(n):
+            c, gi = divmod(n, GROUPS)
+            cols = part(c, CHUNK)
+            codes = flow.tile([P, CHUNK], U32, name="y_codes%d" % n, tag="y_codes", bufs=6, align_bytes=64)
+            scales = y_scale_first[:, cols] if gi == 0 else y_scale_rest[4 * (gi - 1) :, cols]
+            nc.vector.quantize_mx(out=codes[:].bitcast(FP8X4), scales=scales, in_=y_wide[n][:])
+            nc.sync.dma_start(
+                out=out_1[gi].rearrange("p m t -> p (m t)").bitcast(I32)[:, cols], in_=codes[:].bitcast(I32)
+            )
+            if n == UNITS - GROUPS:
+                for quad in range(4):
+                    nc.sync.dma_start(
+                        out=out_2[0, part(quad, 4), :].bitcast(I32),
+                        in_=y_scale_first[32 * quad : 32 * quad + 4, :].bitcast(I32),
+                    )
+            if n == UNITS - 1:
+                for quad in range(4):
+                    queue = nc.scalar if quad % 2 else nc.sync
+                    queue.dma_start(
+                        out=out_2[1:, part(quad, 4), :].bitcast(I32),
+                        in_=y_scale_rest[32 * quad : 32 * quad + 8, :].bitcast(I32),
+                    )
+
+        load_right(0)
+        load_left(0)
+        load_energy(0, 0)
+        nc.sync.dma_start(out=meas[:], in_=measure.rearrange("(g p t) -> p g t", p=P, t=SLOTS))
+        for g in range(1, GROUPS):
+            load_right(g)
+            load_energy(g, 0)
+        load_left(1)
+        for g in range(GROUPS):
+            load_energy(g, 1)
+        nc.sync.dma_start(out=beta_raw[:], in_=half_beta.rearrange("(c q e) -> q c e", q=P, e=2))
+        nc.sync.dma_start(out=c_raw[:].bitcast(I32), in_=c_words[0].rearrange("p n t -> p (n t)").bitcast(I32))
+        load_scale_rows(c_scale_raw, c_scales)
+        load_scale_rows(phi_scale, phi_scales)
+        nc.sync.dma_start(out=phi[:].bitcast(I32), in_=phi_words[0].bitcast(I32))
+        load_left(2)
+
+        arrival = [GROUPS * (2 * h + c) + g for h in range(2) for g in range(GROUPS) for c in range(2)]
+        interleave_right(0)
+        turn_left(0)
+        for step, n in enumerate(arrival):
+            turn_energy(n, 0)
+            inverse_root(n)
+            if step == 0:
+                quantise_right(0)
+                interleave_right(1)
+                quantise_left(0)
+            if step == UNITS // 2 - 1:
+                turn_left(1)
+            kern_up_to(int(KERN_EARLY * (step + 1 - KERN_FIRST_STEP)))
+            if step == 1:
+                quantise_right(1)
+                interleave_right(2)
+            if step == 2:
+                quantise_right(2)
+            if step == UNITS // 2:
+                quantise_left(1)
+            quantise_kern()
+            if step == SORT_STEP:
+                sort_coefficients()
+
+        kern_before = len(kern_made) + KERN_BRIDGE
+        turn_energy(0, 1)
         tanh(0)
         squares_up_to(1)
-        added, rounded, quantised = [], [], []
-        for step in range(steps):
+        for step in range(UNITS + Y_LAG):
             if step + 1 < UNITS:
-                turn_energy(step + 1, "b")
-            if 0 <= step - 2 < UNITS:
+                turn_energy(step + 1, 1)
+            if 2 <= step < UNITS + 2:
                 turn_back(step - 2)
-            if step == L2 - UNITS:
+            if step == 0:
                 turn_left(2)
             if step + 1 < UNITS:
                 tanh(step + 1)
-            if 0 <= step - 2 < UNITS:
+            if 2 <= step < UNITS + 2:
                 copy_back(step - 2)
             if step < UNITS:
-                weight(step)
-            if 0 <= step - 1 < UNITS:
+                pair_weight(step)
+            if 1 <= step < UNITS + 1:
                 weighted_gap(step - 1)
-            squares_up_to(1 + int(SQ_RATE * (step + 1)))
-            before = len(added)
-            for n in plan[step]:
-                new_gap(n)
-                added.append(n)
+            squares_up_to(1 + int(SQUARES * (step + 1)))
+            if step >= Y_LAG:
+                new_gap(step - Y_LAG)
             if step == UNITS + 1:
-                for n in range(UNITS - GROUPS, UNITS - GROUPS + OPEN):
-                    for h in range(2):
-                        open_bank(n, h)
-            if step == L2 - UNITS:
+                for n in range(UNITS - GROUPS, UNITS):
+                    for pair in range(2):
+                        open_y_bank(n, pair)
+            if step == 0:
                 for h in range(2):
-                    for gi in range(GROUPS):
-                        load_source(gi, h)
-            kern_up_to(kern_count[step])
-            if step < UNITS:
-                weight_rest(step)
-            if step == L2 - UNITS:
+                    for g in range(GROUPS):
+                        load_source(g, h)
+            kern_up_to(kern_before + int(KERN_LATE * (step + 1)))
+            if step == 0:
                 quantise_left(2)
-            quantise_finished_kern()
-            for n in rounded[len(quantised) :]:
-                quantise_y(n)
-                quantised.append(n)
-            if 0 <= step - 2 < UNITS:
+            quantise_kern()
+            if step > Y_LAG:
+                quantise_y(step - Y_LAG - 1)
+            if 2 <= step < UNITS + 2:
                 quantise_gap(step - 2)
-            for n in added[len(rounded) : min(int(R_RATE * max(step - R_LAG + 1, 0)), before + R_OFF)]:
-                round_y(n)
-                rounded.append(n)
-        for n in rounded[len(quantised) :]:
-            quantise_y(n)
-        assert len(rounded) == UNITS
+            if step >= Y_LAG:
+                round_y(step - Y_LAG)
+        quantise_y(UNITS - 1)

@@ -26,15 +26,14 @@ HALF = SAMPLES // 2
 UNITS = CHUNKS * GROUPS
 KERN_BANKS = GROUPS * GROUPS * SLOTS
 
-KERN_FIRST_STEP = 2
-KERN_EARLY = 1.8
-KERN_BRIDGE = 3
-KERN_LATE = 2.2
+KERN_FIRST_STEP = 3
+KERN_EARLY = 2
+KERN_BRIDGE = 2
+KERN_LATE = 3
+KERN_BEFORE = KERN_EARLY * (UNITS - KERN_FIRST_STEP)
 SQUARES = 1.5
 SORT_STEP = 9
 Y_LAG = GROUPS + 2
-TANH_BUFS = 3
-WIDE_BUFS = 6
 
 
 def tile_bcs_gap_sweep_k4_kernel(
@@ -60,13 +59,13 @@ def tile_bcs_gap_sweep_k4_kernel(
             return flow.tile([P, SLOTS, GROUP], BF16, name=name, tag="raw", bufs=2 * GROUPS)
 
         def wide_tile(name):
-            return flow.tile([P, SLOTS * GROUP], BF16, name=name, tag="wide", bufs=WIDE_BUFS, align_bytes=64)
+            return flow.tile([P, SLOTS * GROUP], BF16, name=name, tag="wide", bufs=5, align_bytes=64)
 
         def unit_tile(name, shape):
             return flow.tile(shape, F32, name=name, tag="unit", bufs=UNITS + 1)
 
-        def turn_tile(name, dtype):
-            return flow.tile([P, 2 * GROUP], dtype, name=name, tag="turn", bufs=3, align_bytes=64)
+        def turn_tile(name, columns, dtype):
+            return flow.tile([P, columns], dtype, name=name, tag="turn", bufs=3, align_bytes=64)
 
         def rows(ap, g):
             return ap[GROUP * g : GROUP * (g + 1), :].rearrange("(p t) c -> p t c", t=SLOTS)
@@ -147,7 +146,8 @@ def tile_bcs_gap_sweep_k4_kernel(
             quantise(right_q[g], right_wide[g])
 
         def turn_left(g):
-            left_wide[g] = wide_tile("left_wide%d" % g)
+            name = "left_wide%d" % g
+            left_wide[g] = turn_tile(name, SLOTS * GROUP, BF16) if g == GROUPS - 1 else wide_tile(name)
             words = left_raw[g][:].rearrange("p t r -> p (t r)").bitcast(F32)
             for pair in range(2):
                 bank = new_bank("left_bank%d_%d" % (g, pair))
@@ -168,7 +168,9 @@ def tile_bcs_gap_sweep_k4_kernel(
         def kern_bank(b):
             gi, gj, s = b // (GROUPS * SLOTS), b // SLOTS % GROUPS, b % SLOTS
             if s == 0:
-                kern_wide[gj, gi] = wide_tile("kern_wide%d_%d" % (gj, gi))
+                name = "kern_wide%d_%d" % (gj, gi)
+                at_change = b // SLOTS == KERN_BEFORE // SLOTS
+                kern_wide[gj, gi] = turn_tile(name, SLOTS * GROUP, BF16) if at_change else wide_tile(name)
             bank = new_bank("kern_bank%d" % b)
             for t in range(SLOTS):
                 multiply(bank[:, part(t, P)], right_q[gj], part(t, P), left_q[gi], part(s, P), True, True)
@@ -234,7 +236,7 @@ def tile_bcs_gap_sweep_k4_kernel(
                 squared.append(n)
 
         def tanh(n):
-            tanh_sb[n] = flow.tile([P, 2 * GROUP], F32, name="tanh%d" % n, tag="tanh", bufs=TANH_BUFS)
+            tanh_sb[n] = flow.tile([P, 2 * GROUP], F32, name="tanh%d" % n, tag="tanh", bufs=2)
             for e in range(2):
                 nc.scalar.activation(
                     out=in_word_order(tanh_sb[n][:, part(e, GROUP)]),
@@ -244,7 +246,7 @@ def tile_bcs_gap_sweep_k4_kernel(
                 )
 
         def pair_weight(n):
-            chi[n] = turn_tile("chi%d" % n, F32)
+            chi[n] = turn_tile("chi%d" % n, 2 * GROUP, F32)
             nc.gpsimd.tensor_tensor(out=chi[n][:], in0=tanh_sb[n][:], in1=inverse[n][:], op=ALU.mult)
 
         def weighted_gap(n):
@@ -274,7 +276,7 @@ def tile_bcs_gap_sweep_k4_kernel(
                 nc.tensor.transpose(gap_bank[n][:, part(a, P)], gap_t[n][:].bitcast(F32)[:, part(a, P)], ident[:])
 
         def copy_back(n):
-            gap_wide[n] = turn_tile("gap_wide%d" % n, BF16)
+            gap_wide[n] = turn_tile("gap_wide%d" % n, SLOTS * CHUNK, BF16)
             nc.scalar.copy(
                 out=gap_wide[n][:].bitcast(F32).rearrange("p (q a) -> p q a", a=4),
                 in_=gap_bank[n][:].rearrange("p (a q) -> p q a", a=4),
@@ -363,44 +365,45 @@ def tile_bcs_gap_sweep_k4_kernel(
         load_left(2)
 
         arrival = [GROUPS * (2 * h + c) + g for h in range(2) for g in range(GROUPS) for c in range(2)]
-        interleave_right(0)
         turn_left(0)
         for step, n in enumerate(arrival):
             turn_energy(n, 0)
             inverse_root(n)
             if step == 0:
+                interleave_right(0)
                 quantise_right(0)
-                interleave_right(1)
                 quantise_left(0)
-            if step == UNITS // 2 - 1:
-                turn_left(1)
-            kern_up_to(int(KERN_EARLY * (step + 1 - KERN_FIRST_STEP)))
-            if step == 1:
+                interleave_right(1)
                 quantise_right(1)
                 interleave_right(2)
-            if step == 2:
-                quantise_right(2)
             if step == UNITS // 2:
+                turn_left(1)
+            kern_up_to(KERN_EARLY * (step + 1 - KERN_FIRST_STEP))
+            if step == KERN_FIRST_STEP:
+                quantise_right(2)
+            if step == UNITS // 2 + 1:
                 quantise_left(1)
             quantise_kern()
             if step == SORT_STEP:
                 sort_coefficients()
 
-        kern_before = len(kern_made) + KERN_BRIDGE
         turn_energy(0, 1)
         tanh(0)
         squares_up_to(1)
+        y_quantised = []
         for step in range(UNITS + Y_LAG):
-            if step + 1 < UNITS:
-                turn_energy(step + 1, 1)
             if 2 <= step < UNITS + 2:
                 turn_back(step - 2)
+            if step + 1 < UNITS:
+                turn_energy(step + 1, 1)
             if step == 0:
                 turn_left(2)
-            if step + 1 < UNITS:
-                tanh(step + 1)
             if 2 <= step < UNITS + 2:
                 copy_back(step - 2)
+            if step + 1 < UNITS:
+                tanh(step + 1)
+            if step > Y_LAG:
+                round_y(step - Y_LAG - 1)
             if step < UNITS:
                 pair_weight(step)
             if 1 <= step < UNITS + 1:
@@ -409,21 +412,23 @@ def tile_bcs_gap_sweep_k4_kernel(
             if step >= Y_LAG:
                 new_gap(step - Y_LAG)
             if step == UNITS + 1:
-                for n in range(UNITS - GROUPS, UNITS):
+                for n in range(UNITS - GROUPS, UNITS - 1):
                     for pair in range(2):
                         open_y_bank(n, pair)
             if step == 0:
                 for h in range(2):
                     for g in range(GROUPS):
                         load_source(g, h)
-            kern_up_to(kern_before + int(KERN_LATE * (step + 1)))
+            kern_up_to(KERN_BEFORE + KERN_BRIDGE + KERN_LATE * (step + 1))
             if step == 0:
                 quantise_left(2)
-            quantise_kern()
-            if step > Y_LAG:
-                quantise_y(step - Y_LAG - 1)
+            if step != 1:
+                quantise_kern()
             if 2 <= step < UNITS + 2:
                 quantise_gap(step - 2)
-            if step >= Y_LAG:
-                round_y(step - Y_LAG)
+            rounded = len(y_wide) if step >= UNITS else max(len(y_wide) - 1, 0)
+            for n in range(len(y_quantised), rounded):
+                quantise_y(n)
+                y_quantised.append(n)
+        round_y(UNITS - 1)
         quantise_y(UNITS - 1)

from contextlib import ExitStack

import concourse.mybir as mybir
from concourse.masks import make_identity

F32 = mybir.dt.float32
BF16 = mybir.dt.bfloat16
I32 = mybir.dt.int32
U32 = mybir.dt.uint32
U8 = mybir.dt.uint8
FP8X4 = mybir.dt.float8_e4m3fn_x4
FP4X4 = mybir.dt.float4_e2m1fn_x4
ACT = mybir.ActivationFunctionType
ALU = mybir.AluOpType

MOMENTA, SAMPLES, RANK, BASIS = 1536, 1024, 512, 512
FLOPS = 2 * MOMENTA * (MOMENTA * RANK + BASIS * SAMPLES + MOMENTA * SAMPLES)

P = 128
SLOTS = 4
GROUP = P * SLOTS
GROUPS = MOMENTA // GROUP
CHUNK = 2 * P
CHUNKS = SAMPLES // CHUNK
HALF = SAMPLES // 2
UNITS = CHUNKS * GROUPS
KERN_BANKS = GROUPS * GROUPS * SLOTS

KERN_FIRST_STEP = 3
KERN_EARLY = 2
KERN_BRIDGE = 2
KERN_LATE = 3
KERN_BEFORE = KERN_EARLY * (UNITS - KERN_FIRST_STEP)
SQUARES = 1.5
SORT_STEP = 9
Y_LAG = GROUPS + 2


def tile_bcs_gap_sweep_k4_kernel(
    tc, pair_left, pair_right, measure, phi_words, phi_scales, c_words, c_scales, energy, half_beta, source,
    out_0, out_1, out_2,
):
    nc = tc.nc
    with ExitStack() as ctx:
        keep = ctx.enter_context(tc.tile_pool(name="keep", bufs=1))
        flow = ctx.enter_context(tc.tile_pool(name="flow", bufs=1))
        psum = ctx.enter_context(tc.psum_pool(name="psum", bufs=1))
        ctx.enter_context(tc.manual_schedule())

        def new_bank(name):
            return psum.tile([P, GROUP], F32, name=name, tag="ring", bufs=8)

        def new_operand(name, width):
            codes = keep.tile([P, width], U32, name=name + "_codes", align_bytes=64)
            scales = keep.tile([P, width], U8, name=name + "_scales", align_bytes=64)
            return codes, scales

        def raw_tile(name):
            return flow.tile([P, SLOTS, GROUP], BF16, name=name, tag="raw", bufs=2 * GROUPS)

        def wide_tile(name):
            return flow.tile([P, SLOTS * GROUP], BF16, name=name, tag="wide", bufs=5, align_bytes=64)

        def unit_tile(name, shape):
            return flow.tile(shape, F32, name=name, tag="unit", bufs=UNITS + 1)

        def turn_tile(name, columns, dtype):
            return flow.tile([P, columns], dtype, name=name, tag="turn", bufs=3, align_bytes=64)

        def rows(ap, g):
            return ap[GROUP * g : GROUP * (g + 1), :].rearrange("(p t) c -> p t c", t=SLOTS)

        def part(i, size):
            return slice(size * i, size * (i + 1))

        def quantise(operand, values):
            nc.vector.quantize_mx(out=operand[0][:].bitcast(FP8X4), scales=operand[1][:], in_=values[:])

        def multiply(out, stationary, stationary_cols, moving, moving_cols, start, stop):
            nc.tensor.matmul_mx(
                out=out,
                lhsT=stationary[0][:, stationary_cols].bitcast(FP8X4),
                lhsT_scale=stationary[1][:, stationary_cols],
                rhs=moving[0][:, moving_cols].bitcast(FP8X4),
                rhs_scale=moving[1][:, moving_cols],
                start=start,
                stop=stop,
            )

        ident = keep.tile([P, P], F32, name="ident")
        make_identity(nc, ident[:])
        phi_scale = keep.tile([P, MOMENTA], U8, name="phi_scale", align_bytes=64)
        c_scale_raw = keep.tile([P, SAMPLES], U8, name="c_scale_raw", align_bytes=64)
        nc.gpsimd.memset(phi_scale[:].bitcast(I32), 0)
        nc.gpsimd.memset(c_scale_raw[:].bitcast(I32), 0)

        meas = keep.tile([P, GROUPS, SLOTS], BF16, name="meas")
        beta_raw = keep.tile([P, CHUNKS, 2], BF16, name="beta_raw")
        beta = keep.tile([P, CHUNKS * 2], F32, name="beta")
        phi = keep.tile([P, 2 * MOMENTA], U8, name="phi", align_bytes=64)
        c_raw = keep.tile([P, SAMPLES], U32, name="c_raw", align_bytes=64)
        coef = new_operand("coef", SAMPLES)
        y_scale_first = keep.tile([P, SAMPLES], U8, name="y_scale_first", align_bytes=64)
        y_scale_rest = keep.tile([P, SAMPLES], U8, name="y_scale_rest", align_bytes=64)

        right_raw, right_wide, right_q = {}, {}, {}
        left_raw, left_wide, left_q = {}, {}, {}
        kern_wide, kern_q = {}, {}
        energy_sb, energy_t, inverse, tanh_sb, chi = {}, {}, {}, {}, {}
        gap_t, gap_bank, gap_wide, gap_q = {}, {}, {}, {}
        source_sb, y_bank, y_sb, y_wide = {}, {}, {}, {}


        def load_right(g):
            right_raw[g] = raw_tile("right_raw%d" % g)
            nc.sync.dma_start(out=right_raw[g][:], in_=rows(pair_right[:, part(g, GROUP)], 0))

        def load_left(g):
            left_raw[g] = raw_tile("left_raw%d" % g)
            nc.sync.dma_start(out=left_raw[g][:], in_=rows(pair_left, g))

        def load_energy(g, h):
            energy_sb[g, h] = keep.tile([P, SLOTS, HALF], BF16, name="energy%d_%d" % (g, h))
            nc.sync.dma_start(out=energy_sb[g, h][:], in_=rows(energy[:, part(h, HALF)], g))

        def load_source(g, h):
            source_sb[g, h] = raw_tile("source%d_%d" % (g, h))
            nc.sync.dma_start(out=source_sb[g, h][:], in_=rows(source[:, part(h, HALF)], g))

        def load_scale_rows(tile, scales):
            for quad in range(4):
                nc.sync.dma_start(
                    out=tile[32 * quad : 32 * quad + 4, :].bitcast(I32), in_=scales[0, part(quad, 4), :].bitcast(I32)
                )


        def interleave_right(g):
            right_wide[g] = wide_tile("right_wide%d" % g)
            nc.vector.tensor_copy(
                out=right_wide[g][:].rearrange("p (t a b s) -> p a t b s", t=SLOTS, b=2, s=SLOTS),
                in_=right_raw[g][:].rearrange("p s (a b t) -> p a t b s", b=2, t=SLOTS),
            )

        def quantise_right(g):
            right_q[g] = new_operand("right%d" % g, GROUP)
            quantise(right_q[g], right_wide[g])

        def turn_left(g):
            name = "left_wide%d" % g
            left_wide[g] = turn_tile(name, SLOTS * GROUP, BF16) if g == GROUPS - 1 else wide_tile(name)
            words = left_raw[g][:].rearrange("p t r -> p (t r)").bitcast(F32)
            for pair in range(2):
                bank = new_bank("left_bank%d_%d" % (g, pair))
                for a in range(4):
                    t, u = 2 * pair + a // 2, a % 2
                    nc.tensor.transpose(
                        bank[:, part(a, P)], words[:, RANK // 2 * t + u : RANK // 2 * (t + 1) : 2], ident[:]
                    )
                nc.scalar.copy(
                    out=left_wide[g][:].bitcast(F32)[:, part(pair, GROUP)].rearrange("p (t i u) -> p t i u", t=2, u=2),
                    in_=bank[:].rearrange("p (t u i) -> p t i u", t=2, u=2),
                )

        def quantise_left(g):
            left_q[g] = new_operand("left%d" % g, GROUP)
            quantise(left_q[g], left_wide[g])

        def kern_bank(b):
            gi, gj, s = b // (GROUPS * SLOTS), b // SLOTS % GROUPS, b % SLOTS
            if s == 0:
                name = "kern_wide%d_%d" % (gj, gi)
                at_change = b // SLOTS == KERN_BEFORE // SLOTS
                kern_wide[gj, gi] = turn_tile(name, SLOTS * GROUP, BF16) if at_change else wide_tile(name)
            bank = new_bank("kern_bank%d" % b)
            for t in range(SLOTS):
                multiply(bank[:, part(t, P)], right_q[gj], part(t, P), left_q[gi], part(s, P), True, True)
            nc.vector.tensor_tensor(
                out=kern_wide[gj, gi][:, part(s, GROUP)].rearrange("p (i t) -> p i t", t=SLOTS),
                in0=bank[:].rearrange("p (t i) -> p i t", t=SLOTS),
                in1=meas[:, gj, :].unsqueeze(1).to_broadcast([P, P, SLOTS]),
                op=ALU.mult,
            )

        kern_made = []

        def kern_up_to(count):
            for b in range(len(kern_made), min(count, KERN_BANKS)):
                kern_bank(b)
                kern_made.append(b)

        def quantise_kern():
            made = len(kern_made)
            for tile in range(len(kern_q), made // SLOTS if made == KERN_BANKS else max(made - 1, 0) // SLOTS):
                gi, gj = divmod(tile, GROUPS)
                kern_q[gj, gi] = new_operand("kern%d_%d" % (gj, gi), GROUP)
                quantise(kern_q[gj, gi], kern_wide[gj, gi])


        def sort_coefficients():
            nc.vector.tensor_copy(out=beta[:], in_=beta_raw[:].rearrange("q c e -> q (c e)"))
            nc.vector.tensor_copy(
                out=coef[0][:].bitcast(I32).rearrange("p (c e a b) -> p c a e b", c=CHUNKS, e=2, b=4),
                in_=c_raw[:].bitcast(I32).rearrange("p (c a b e) -> p c a e b", c=CHUNKS, e=2, b=4),
            )
            nc.vector.tensor_copy(
                out=coef[1][:].rearrange("p (c e a b) -> p c a e b", c=CHUNKS, e=2, b=16),
                in_=c_scale_raw[:].rearrange("p (c a b e) -> p c a e b", c=CHUNKS, e=2, b=16),
            )

        def in_word_order(ap):
            return ap.rearrange("q (u p b) -> q u p b", u=2, b=2)

        def turn_energy(n, phase):
            c, g = divmod(n, GROUPS)
            words = energy_sb[g, c // 2][:].rearrange("p t m -> p (t m)").bitcast(F32)
            bank = new_bank("energy_bank%d_%d" % (phase, n))
            for t in range(SLOTS):
                nc.tensor.transpose(bank[:, part(t, P)], words[:, part(2 * t + c % 2, P)], ident[:])
            energy_t[n] = bank[:].bitcast(BF16).rearrange("q (u b p e) -> q e u p b", u=2, b=2, e=2)

        def inverse_root(n):
            inverse[n] = unit_tile("inverse%d" % n, [P, 2 * GROUP])
            for e in range(2):
                nc.scalar.activation(
                    out=in_word_order(inverse[n][:, part(e, GROUP)]),
                    in_=energy_t[n][:, e, :, :, :],
                    func=ACT.Abs_reciprocal_sqrt,
                    scale=2.0,
                )

        squared = []

        def squares_up_to(count):
            for n in range(len(squared), min(count, UNITS)):
                nc.scalar.activation(out=inverse[n][:], in_=inverse[n][:], func=ACT.Square)
                squared.append(n)

        def tanh(n):
            tanh_sb[n] = flow.tile([P, 2 * GROUP], F32, name="tanh%d" % n, tag="tanh", bufs=2)
            for e in range(2):
                nc.scalar.activation(
                    out=in_word_order(tanh_sb[n][:, part(e, GROUP)]),
                    in_=energy_t[n][:, e, :, :, :],
                    func=ACT.Tanh,
                    scale=beta[:, part(2 * (n // GROUPS) + e, 1)],
                )

        def pair_weight(n):
            chi[n] = turn_tile("chi%d" % n, 2 * GROUP, F32)
            nc.gpsimd.tensor_tensor(out=chi[n][:], in0=tanh_sb[n][:], in1=inverse[n][:], op=ALU.mult)

        def weighted_gap(n):
            c, g = divmod(n, GROUPS)
            gap_t[n] = flow.tile([P, 2 * GROUP], BF16, name="gap_t%d" % n, tag="gap_t", bufs=2)
            for e in range(2):
                bank = new_bank("delta_bank%d_%d" % (n, e))
                nc.tensor.matmul_mx(
                    out=bank[:],
                    lhsT=coef[0][:, part(2 * c + e, P)].bitcast(FP8X4),
                    lhsT_scale=coef[1][:, part(2 * c + e, P)],
                    rhs=phi[:, part(g, 2 * GROUP)].bitcast(FP4X4),
                    rhs_scale=phi_scale[:, part(g, GROUP)],
                    start=True,
                    stop=True,
                )
                nc.vector.tensor_tensor(
                    out=in_word_order(gap_t[n][:, part(e, GROUP)]),
                    in0=bank[:].rearrange("q (p u b) -> q u p b", u=2, b=2),
                    in1=in_word_order(chi[n][:, part(e, GROUP)]),
                    op=ALU.mult,
                )

        def turn_back(n):
            gap_bank[n] = new_bank("gap_bank%d" % n)
            for a in range(4):
                nc.tensor.transpose(gap_bank[n][:, part(a, P)], gap_t[n][:].bitcast(F32)[:, part(a, P)], ident[:])

        def copy_back(n):
            gap_wide[n] = turn_tile("gap_wide%d" % n, SLOTS * CHUNK, BF16)
            nc.scalar.copy(
                out=gap_wide[n][:].bitcast(F32).rearrange("p (q a) -> p q a", a=4),
                in_=gap_bank[n][:].rearrange("p (a q) -> p q a", a=4),
            )

        def quantise_gap(n):
            gap_q[n] = new_operand("gap%d" % n, CHUNK)
            quantise(gap_q[n], gap_wide[n])


        def y_pass(n, t, gj):
            c, gi = divmod(n, GROUPS)
            multiply(
                y_bank[n, t // 2][:, part(t % 2, CHUNK)], kern_q[gj, gi], part(t, P), gap_q[GROUPS * c + gj],
                part(0, CHUNK), gj == 0, gj == GROUPS - 1,
            )

        def open_y_bank(n, pair):
            y_bank[n, pair] = new_bank("y_bank%d_%d" % (n, pair))
            for gj in range(GROUPS - 1):
                y_pass(n, 2 * pair, gj)

        def new_gap(n):
            c, gi = divmod(n, GROUPS)
            y_sb[n] = unit_tile("y%d" % n, [P, SLOTS, CHUNK])
            for pair in range(2):
                if (n, pair) not in y_bank:
                    open_y_bank(n, pair)
                y_pass(n, 2 * pair, GROUPS - 1)
                for gj in range(GROUPS):
                    y_pass(n, 2 * pair + 1, gj)
                nc.vector.tensor_tensor(
                    out=y_sb[n][:, part(pair, 2), :],
                    in0=y_bank[n, pair][:].rearrange("p (t m) -> p t m", t=2),
                    in1=source_sb[gi, c // 2][:, part(pair, 2), part(c % 2, CHUNK)],
                    op=ALU.add,
                )
            nc.sync.dma_start(out=rows(out_0[:, part(c, CHUNK)], gi), in_=y_sb[n][:])

        def round_y(n):
            y_wide[n] = flow.tile([P, SLOTS * CHUNK], BF16, name="y_wide%d" % n, tag="y_wide", bufs=3, align_bytes=64)
            copy = nc.vector.tensor_copy if n == UNITS - 1 else nc.scalar.copy
            copy(
                out=y_wide[n][:].rearrange("p (a b t) -> p a t b", b=2, t=SLOTS),
                in_=y_sb[n][:].rearrange("p t (a b) -> p a t b", b=2),
            )

        def quantise_y(n):
            c, gi = divmod(n, GROUPS)
            cols = part(c, CHUNK)
            codes = flow.tile([P, CHUNK], U32, name="y_codes%d" % n, tag="y_codes", bufs=6, align_bytes=64)
            scales = y_scale_first[:, cols] if gi == 0 else y_scale_rest[4 * (gi - 1) :, cols]
            nc.vector.quantize_mx(out=codes[:].bitcast(FP8X4), scales=scales, in_=y_wide[n][:])
            nc.sync.dma_start(
                out=out_1[gi].rearrange("p m t -> p (m t)").bitcast(I32)[:, cols], in_=codes[:].bitcast(I32)
            )
            if n == UNITS - GROUPS:
                for quad in range(4):
                    nc.sync.dma_start(
                        out=out_2[0, part(quad, 4), :].bitcast(I32),
                        in_=y_scale_first[32 * quad : 32 * quad + 4, :].bitcast(I32),
                    )
            if n == UNITS - 1:
                for quad in range(4):
                    queue = nc.scalar if quad % 2 else nc.sync
                    queue.dma_start(
                        out=out_2[1:, part(quad, 4), :].bitcast(I32),
                        in_=y_scale_rest[32 * quad : 32 * quad + 8, :].bitcast(I32),
                    )

        load_right(0)
        load_left(0)
        load_energy(0, 0)
        nc.sync.dma_start(out=meas[:], in_=measure.rearrange("(g p t) -> p g t", p=P, t=SLOTS))
        for g in range(1, GROUPS):
            load_right(g)
            load_energy(g, 0)
        load_left(1)
        for g in range(GROUPS):
            load_energy(g, 1)
        nc.sync.dma_start(out=beta_raw[:], in_=half_beta.rearrange("(c q e) -> q c e", q=P, e=2))
        nc.sync.dma_start(out=c_raw[:].bitcast(I32), in_=c_words[0].rearrange("p n t -> p (n t)").bitcast(I32))
        load_scale_rows(c_scale_raw, c_scales)
        load_scale_rows(phi_scale, phi_scales)
        nc.sync.dma_start(out=phi[:].bitcast(I32), in_=phi_words[0].bitcast(I32))
        load_left(2)

        arrival = [GROUPS * (2 * h + c) + g for h in range(2) for g in range(GROUPS) for c in range(2)]
        turn_left(0)
        for step, n in enumerate(arrival):
            turn_energy(n, 0)
            inverse_root(n)
            if step == 0:
                interleave_right(0)
                quantise_right(0)
                quantise_left(0)
                interleave_right(1)
                quantise_right(1)
                interleave_right(2)
            if step == UNITS // 2:
                turn_left(1)
            kern_up_to(KERN_EARLY * (step + 1 - KERN_FIRST_STEP))
            if step == KERN_FIRST_STEP:
                quantise_right(2)
            if step == UNITS // 2 + 1:
                quantise_left(1)
            quantise_kern()
            if step == SORT_STEP:
                sort_coefficients()

        turn_energy(0, 1)
        tanh(0)
        squares_up_to(1)
        y_quantised = []
        for step in range(UNITS + Y_LAG):
            if 2 <= step < UNITS + 2:
                turn_back(step - 2)
            if step + 1 < UNITS:
                turn_energy(step + 1, 1)
            if step == 0:
                turn_left(2)
            if 2 <= step < UNITS + 2:
                copy_back(step - 2)
            if step + 1 < UNITS:
                tanh(step + 1)
            if step > Y_LAG:
                round_y(step - Y_LAG - 1)
            if step < UNITS:
                pair_weight(step)
            if 1 <= step < UNITS + 1:
                weighted_gap(step - 1)
            squares_up_to(1 + int(SQUARES * (step + 1)))
            if step >= Y_LAG:
                new_gap(step - Y_LAG)
            if step == UNITS + 1:
                for n in range(UNITS - GROUPS, UNITS - 1):
                    for pair in range(2):
                        open_y_bank(n, pair)
            if step == 0:
                for h in range(2):
                    for g in range(GROUPS):
                        load_source(g, h)
            kern_up_to(KERN_BEFORE + KERN_BRIDGE + KERN_LATE * (step + 1))
            if step == 0:
                quantise_left(2)
            if step != 1:
                quantise_kern()
            if 2 <= step < UNITS + 2:
                quantise_gap(step - 2)
            rounded = len(y_wide) if step >= UNITS else max(len(y_wide) - 1, 0)
            for n in range(len(y_quantised), rounded):
                quantise_y(n)
                y_quantised.append(n)
        round_y(UNITS - 1)
        quantise_y(UNITS - 1)
